import numpy as np
CORES = [129,145,193,257,273,321,385,401,449]
N = 9
T, EL, CAP, CAPP = 512, 2, 240, 64
E = N * EL
def entries(a): return a.T.reshape(-1)
def pack(v, P): return np.ascontiguousarray(np.asarray(v, np.int32).reshape(-1, P).T)
def lists(rng, how):
    if how == "uniform": return {"ex": np.stack([pack(rng.permutation(np.repeat(np.arange(E), CAPP))[:T], 16) for r in range(N)])}
    R = np.arange(N)[:, None]; c = rng.permutation(E); C = np.zeros((N, E), np.int64)
    if how == "bands":
        a = c % N; C = CAPP * ((R >= a) & (R <= a + CAP // CAPP)); C[a, np.arange(E)] = np.where(c < N, CAPP, rng.integers(1, CAPP + 1, E))
    if how == "full":
        g = T // CAPP; C[:, c[:g]] = CAPP; C[:, c[:g // 2]] = rng.integers(CAPP // 2, CAPP + 1, (N, g // 2))
    if how in ("skew", "sorted"):
        V = np.full((N, 3), CAP // N); V[:, 0] = rng.integers(2, CAP // N + 1, N); h = rng.integers(1, N - 2); V[h, 0] = 0; V[h + 1, 0] = 1; V[rng.integers(N), 1:] += CAP % N; V[rng.integers(N), 2] += 1
        W = rng.random((N, E)) ** 4 + 1e-9; W[:, c[:3]] = 0
        C = np.minimum(((T - T // 8 - V.sum(axis=1, keepdims=True)) * W / W.sum(axis=1, keepdims=True)).astype(np.int64), CAPP); C[:, c[:3]] = V
    if how == "thin":
        C = rng.integers(0, CAP // N + 1, (N, E)); C[1] = 1; C[[0, N // 2, N - 1]] = 0
    X = np.stack([rng.permutation(np.concatenate([np.repeat(np.arange(E), C[r]), np.full(T - C[r].sum(), -1)])) for r in range(N)])
    if how == "sorted": X = np.sort(X, axis=1); X[1::2] = X[1::2, ::-1].copy()
    return {"ex": np.stack([pack(v, 16) for v in X])}
def blank(d):
    for r in range(0, N, 2):
        u, i = np.unique(entries(d["ex"][r])[::-1], return_index=True); d["x"][r][:, T - 1 - i[u >= 0]] = 0
def setup_inputs(rng):
    return dict({"x": rng.standard_normal((N, 128, T), dtype=np.float32)}, **lists(rng, "uniform"))
def setup_inputs_bands(rng):
    d = setup_inputs(rng); d.update(lists(rng, "bands"))
    for k in ("x",): d[k] = (d[k].astype(np.float32) * 1048576.0).astype(d[k].dtype)
    blank(d)
    return d
def setup_inputs_full(rng):
    d = setup_inputs(rng); d.update(lists(rng, "full"))
    for k in ("x",): d[k] = (d[k].astype(np.float32) * (1 / 1024.0)).astype(d[k].dtype)
    blank(d)
    return d
def setup_inputs_skew(rng):
    d = setup_inputs(rng); d.update(lists(rng, "skew"))
    blank(d)
    return d
def setup_inputs_sorted(rng):
    d = setup_inputs(rng); d.update(lists(rng, "sorted"))
    blank(d)
    return d
def setup_inputs_thin(rng):
    d = setup_inputs(rng); d.update(lists(rng, "thin"))
    blank(d)
    return d
def check_inputs(x):
    bad = []
    if x["ex"].min() < -1 or x["ex"].max() >= E: bad.append("ex out of range")
    if max(int(np.bincount(entries(a)[entries(a) >= 0], minlength=E).max()) for a in x["ex"]) > CAPP: bad.append("more than CAPP tokens of one rank choose one expert")
    return bad
def reference(x, ex):
    X = np.concatenate(list(x), axis=1); e = np.concatenate([entries(a) for a in ex])
    k = np.nonzero(e >= 0)[0]; o = k[np.argsort(e[k], kind="stable")]; s = e[o]
    p = np.arange(len(o)) - np.searchsorted(s, s)
    Y = np.zeros((128, E * CAP), x.dtype); m = p < CAP; Y[:, CAP * s[m] + p[m]] = X[:, o[m]]
    return {"y": np.stack([Y[:, EL * CAP * r:EL * CAP * (r + 1)] for r in range(N)])}

@@ -1,0 +1,303 @@
+import numpy as np
+from concourse.bass import DstId, RemoteDMATransfer
+from concourse.mybir import AluOpType, ActivationFunctionType, AxisListType
+
+N, EL, CAP = 9, 2, 240
+BLK = 128
+ZERO = N * BLK
+NAG = 3
+MAGIC = 1.5 * 2.0 ** 28
+BIG = 4096.0
+
+SCRATCH = {
+    "E4": ("sbuf", [128, 4], "int32"),
+    "X": ("sbuf", [128, 512], "float32"),
+    "PACK": ("sbuf", [128, 6 * BLK], "float32"),
+    "LAND": ("sbuf", [128, ZERO + 4], "float32"),
+    "Y0": ("sbuf", [128, CAP], "float32"),
+    "Y1": ("sbuf", [128, CAP], "float32"),
+    "EXL": ("dram", [N, 128, 4], "int32"),
+    "EXS": ("sbuf", [72, 64], "int32"),
+    "pco": ("sbuf", [128, 1], "int32"), "ai": ("sbuf", [128, 1], "int32"), "qi": ("sbuf", [128, 1], "int32"),
+    "a16": ("sbuf", [128, 1], "float32"), "a16p": ("sbuf", [128, 1], "float32"), "a64": ("sbuf", [128, 1], "float32"),
+    "kc": ("sbuf", [128, 1], "float32"), "jt": ("sbuf", [128, 4], "float32"),
+    "kap": ("sbuf", [128, 128], "bfloat16"), "kro": ("sbuf", [128, 18], "bfloat16"), "krk": ("sbuf", [1, 72], "bfloat16"),
+    "m15": ("sbuf", [1, 72], "bfloat16"), "aro": ("sbuf", [128, 128], "bfloat16"), "bro": ("sbuf", [128, 72], "bfloat16"),
+    "onb": ("sbuf", [1, 128], "bfloat16"), "msk": ("sbuf", [128, 72], "float32"),
+    "meq": ("sbuf", [128, 128], "bfloat16"), "dia": ("sbuf", [128, 128], "bfloat16"),
+    "mle": ("sbuf", [128, 128], "bfloat16"), "mlt": ("sbuf", [128, 128], "bfloat16"),
+    "e4f": ("sbuf", [128, 4], "float32"), "oh": ("sbuf", [128, 72], "bfloat16"), "sc": ("sbuf", [128, 72], "float32"),
+    "hh": ("sbuf", [128, 4], "float32"), "lo": ("sbuf", [128, 4], "float32"),
+    "bm": ("sbuf", [128, 288], "float16"), "am": ("sbuf", [128, 512], "float16"), "lst": ("sbuf", [128, 72], "uint16"),
+    "onf": ("sbuf", [72, 16], "float32"), "gro": ("sbuf", [128, 128], "bfloat16"), "qif": ("sbuf", [128, 1], "float32"),
+    "mcu": ("sbuf", [72, 128], "float32"), "mcn": ("sbuf", [72, 128], "float32"),
+    "prow": ("sbuf", [128, 32], "float32"), "pc": ("sbuf", [128, 32], "float32"), "brow": ("sbuf", [1, 32], "bfloat16"),
+    "qci": ("sbuf", [128, 1], "int32"), "qcf": ("sbuf", [128, 1], "float32"), "qc2": ("sbuf", [128, 1], "float32"),
+    "rr": ("sbuf", [128, 128], "bfloat16"), "ohr": ("sbuf", [72, 128], "float32"), "cn": ("sbuf", [72, 2], "float32"),
+    "wn": ("sbuf", [128, 2], "float32"), "th": ("sbuf", [128, 32], "bfloat16"), "th9": ("sbuf", [16, 32], "bfloat16"),
+    "yl": ("sbuf", [128, 32], "uint16"),
+    "psP": ("psum", [128, 512], "float32"), "psG": ("psum", [128, 512], "float32"),
+    "psC": ("psum", [128, 512], "float32"), "psO": ("psum", [128, 512], "float32"),
+}
+_K = ["pk%d" % i for i in range(7)]
+_AB = ["ab%d" % i for i in range(4)]
+SEMAPHORES = (["le4", "lx", "lex", "lexs", "ls", "e4a", "xa", "exa", "arr", "sty0", "sty1", "yg0", "yg1"]
+              + ["v%d" % i for i in range(16)] + ["r%d" % i for i in range(10)] + ["g%d" % i for i in range(8)]
+              + ["p%d" % i for i in range(4)] + _K + _AB)
+
+
+def plan(topo, cores):
+    out = []
+    for r, c in enumerate(cores):
+        far = [d for d in range(N) if topo.rack(topo.host(cores[d])) != topo.rack(topo.host(c))]
+        far.sort(key=lambda d: (topo.may_write(c, cores[d]), d))
+        ag = far[:NAG]
+        cand = [k for k in range(512) if topo.rack(topo.host(k)) != topo.rack(topo.host(c)) and topo.may_write(c, k)
+                and topo.chip(k) == topo.chip(c) and topo.die(k) != topo.die(c) and k not in cores
+                and all(topo.may_write(k, cores[d]) for d in ag)]
+        rot = lambda ds: sorted(ds, key=lambda d: (d - r) % N)
+        out.append({"agent": cand[0], "direct": rot([d for d in range(N) if d != r and d not in ag]), "via": rot(ag)})
+    return out
+
+
+def rank_program(g, core, T, topo):
+    cores = list(T.cores)
+    P = plan(topo, cores)
+    rank = T.rank_of(core)
+    agents = {p["agent"]: s for s, p in enumerate(P)}
+    if rank is None and core not in agents:
+        return
+    is_rank = rank is not None
+    src = rank if is_rank else agents[core]
+    dests = P[src]["direct"] if is_rank else P[src]["via"]
+    outs = [cores[d] for d in dests] + ([P[src]["agent"]] if is_rank else [])
+    em = 0xFFFF
+    for o in outs:
+        em = em & topo.mask(core, o)
+    ne = bin(em).count("1")
+
+    V, S, PE, Y = g.vector, g.scalar, g.tensor, g.sync
+    A = AluOpType
+    Copy = ActivationFunctionType.Copy
+    AX = AxisListType.X
+    cnt, seen = {}, {}
+
+    def inc(ins, name, n=1):
+        ins.then_inc(T.sem[name], n)
+        cnt[name] = cnt.get(name, 0) + n
+
+    def wait(q, *names):
+        for name in names:
+            q.wait_ge(T.sem[name], cnt[name])
+            seen[name] = cnt[name]
+
+    def expect(name, n):
+        cnt[name] = cnt.get(name, 0) + n
+
+    def rdma(dst, out_ap, in_ap, sem):
+        rid, pid = topo.addr(dst, core)
+        g.remote_dma(out_ap=out_ap, in_ap=in_ap, remote_sem=T.sem[sem], local_sem=T.sem["ls"], pid=pid, routing_id=rid,
+                     dma_engine_mask=em)
+        expect("ls", ne)
+
+    def send_lists(ds):
+        ids, aps = [], []
+        for d in ds:
+            rid, pid = topo.addr(d, core)
+            ids.append(DstId(rid=rid, pnc=pid))
+            aps.append(T["EXL"][src])
+        g.remote_dma_fused([RemoteDMATransfer(dst_ids=ids, dma_engine_mask=em, remote_sem=T.sem["exa"], srcs=[T["EXL"][src]],
+                                              dsts=aps, alu_op=0)], local_sem=T.sem["ls"])
+        expect("ls", ne)
+
+    def iota(name, pattern, base, mult, sem):
+        inc(g.iota(T[name][:], pattern, base, mult, allow_small_or_imprecise_dtypes=True), sem)
+
+    def ts(sem, out, in0, s1, op0, s2=None, op1=None):
+        if op1 is None:
+            inc(V.tensor_scalar(out, in0, s1, None, op0), sem)
+        else:
+            inc(V.tensor_scalar(out, in0, s1, s2, op0, op1), sem)
+
+    if is_rank:
+        expect("exa", (N - 1) * ne)
+        expect("arr", (N - 1) * ne)
+        inc(Y.dma_start(T["E4"][:], T["ex"][:]), "le4", 16)
+        inc(S.dma_start(T["X"][:], T["x"][:]), "lx", 16)
+        inc(Y.dma_start(T["EXL"][rank], T["ex"][:]), "lex", 16)
+        e4sem, xsem = "le4", "lx"
+    else:
+        expect("e4a", ne)
+        expect("xa", ne)
+        expect("exa", ne)
+        e4sem, xsem = "e4a", "xa"
+
+    inc(g.iota(T["pco"][:], [[0, 1]], 0, 1), "g0")
+    iota("kap", [[1, 16], [16, 8]], 0, 0, "g1")
+    iota("kro", [[1, 18]], 0, 0, "g2")
+    iota("krk", [[0, 4], [128, 18]], 128, 0, "g3")
+    iota("bro", [[32, 72]], int(BIG) + 128, 0, "g4")
+    iota("aro", [[0, 8], [2, 16]], -15, 0, "g5")
+
+    inc(V.memset(T["onb"][:], 1.0), "v0")
+    inc(V.memset(T["m15"][:], -15.0), "v0")
+    inc(V.memset(T["msk"][:], 1.0), "v1")
+    if is_rank:
+        inc(V.memset(T["onf"][:], 1.0), "r0")
+        inc(V.memset(T["LAND"][:, ZERO:ZERO + 4], 0.0), "r0")
+    wait(V, "g0")
+    ts("v2", T["ai"][:], T["pco"][:], 7, A.bitwise_and)
+    ts("v2", T["qi"][:], T["pco"][:], 3, A.arith_shift_right)
+    wait(V, "v1")
+    inc(V.memset(T["msk"][:, 0:72:18], 0.0), "v3")
+    wait(V, "v2")
+    ts("v4", T["a16"][:], T["ai"][:], 16.0, A.mult)
+    ts("v4", T["a16p"][:], T["ai"][:], 16.0, A.mult, 16.0, A.add)
+    ts("v4", T["a64"][:], T["ai"][:], 64.0, A.mult)
+    wait(V, "v4")
+    ts("v5", T["kc"][:], T["qi"][:], T["a16"][:], A.add)
+    for i in range(4):
+        ts("v8", T["jt"][:, i:i + 1], T["qi"][:], T["a64"][:], A.add, 16.0 * i, A.add)
+    wait(V, "v5", "g1")
+    ts("v6", T["meq"][:], T["kap"][:], T["kc"][:], A.is_gt, 2.0, A.mult)
+    ts("v6", T["dia"][:], T["kap"][:], T["kc"][:], A.is_equal, BIG, A.mult)
+    ts("v6", T["mle"][:], T["kap"][:], T["a16"][:], A.is_ge, 2.0, A.mult)
+    ts("v6", T["mlt"][:], T["kap"][:], T["a16p"][:], A.is_ge, 2.0, A.mult)
+
+    if is_rank:
+        ag = P[rank]["agent"]
+        wait(g, "le4")
+        rdma(ag, T["E4"][:], T["E4"][:], "e4a")
+        wait(g, "lx")
+        rdma(ag, T["X"][:], T["X"][:], "xa")
+        wait(g, "lex")
+        send_lists([ag] + [cores[d] for d in dests])
+        iota("gro", [[1, 8], [0, 16]], 0, 0, "g6")
+        iota("prow", [[0, 2], [16, 16]], 0, 0, "g6")
+        iota("brow", [[64, 2], [16, 16]], 0, 0, "g6")
+    else:
+        wait(g, "exa")
+        send_lists([cores[d] for d in dests])
+
+    wait(V, e4sem)
+    inc(V.tensor_copy(T["e4f"][:], T["E4"][:]), "v9")
+    wait(V, "v9", "g2")
+    for i in range(4):
+        ts("v10", T["oh"][:, 18 * i:18 * i + 18], T["kro"][:], T["e4f"][:, i:i + 1], A.is_equal)
+    ps, oh = T["psP"], T["oh"]
+    wait(PE, "v0", "g3")
+    PE.matmul(ps[:, 0:72], T["onb"][:], T["krk"][:], True, False)
+    PE.matmul(ps[:, 0:72], T["onb"][:], T["m15"][:], False, False)
+    wait(PE, "v6", "v10")
+    for n in (1, 2, 3):
+        PE.matmul(ps[:, 18 * n:72], T["mle"][:], oh[:, 0:72 - 18 * n], False, False)
+    for n in (1, 2, 3):
+        PE.matmul(ps[:, 0:72 - 18 * n], T["mlt"][:], oh[:, 18 * n:72], False, False)
+    PE.matmul(ps[:, 0:72], T["meq"][:], oh[:], False, False)
+    inc(PE.matmul(ps[:, 0:72], T["dia"][:], oh[:], False, True), "p0")
+    wait(V, "p0", "v3")
+    inc(V.tensor_tensor_scan(T["sc"][:], T["msk"][:], ps[:, 0:72], 0.0, A.mult, A.max), "v11")
+    wait(V, "v11")
+    ts("v12", T["hh"][:], T["sc"][:, 17:72:18], MAGIC, A.add, MAGIC, A.subtract)
+    wait(V, "v12", "v8", "g4", "g5")
+    inc(V.tensor_tensor(T["lo"][:], T["sc"][:, 17:72:18], T["hh"][:], A.subtract), "v13")
+
+    def bmat(i):
+        ts(_AB[i], T["bm"][:, 72 * i:72 * i + 72], T["bro"][:], T["hh"][:, i:i + 1], A.is_equal, T["jt"][:, i:i + 1], A.mult)
+
+    bmat(0)
+    bmat(1)
+    wait(V, "v13")
+    for i in range(4):
+        ts(_AB[i], T["am"][:, 128 * i:128 * i + 128], T["aro"][:], T["lo"][:, i:i + 1], A.is_equal)
+        if i + 2 < 4:
+            bmat(i + 2)
+    pg = T["psG"]
+    for i in range(4):
+        wait(PE, _AB[i])
+        m = PE.matmul(pg[:, 0:72], T["am"][:, 128 * i:128 * i + 128], T["bm"][:, 72 * i:72 * i + 72], i == 0, i == 3)
+    inc(m, "p1")
+    wait(V, "p1")
+    inc(V.tensor_copy(T["lst"][:], pg[:, 0:72]), "v14")
+
+    def off(d, h=None):
+        return T["lst"][:, 8 * d:8 * d + 8] if h is None else T["lst"][:, 8 * d + 4 * h:8 * d + 4 * h + 4]
+
+    def vget(out, offs, sem):
+        inc(V.tensor_copy(out, T["X"][:].indirect(offs)), sem)
+
+    def sget(out, offs, sem):
+        inc(S.activation(out, T["X"][:].indirect(offs), Copy, bias=-0.0), sem)
+
+    wait(V, "v14", xsem)
+    wait(S, "v14", xsem)
+    pk = T["PACK"]
+    for n, d in enumerate(dests):
+        o = pk[:, BLK * n:BLK * n + BLK]
+        if is_rank or n < 2:
+            (vget if n % 2 == 0 else sget)(o, off(d), _K[n])
+        else:
+            vget(pk[:, BLK * n:BLK * n + 64], off(d, 0), _K[n])
+            sget(pk[:, BLK * n + 64:BLK * n + 128], off(d, 1), _K[n])
+    if is_rank:
+        sget(T["LAND"][:, BLK * rank:BLK * rank + BLK], off(rank), "pk6")
+    for n, d in enumerate(dests):
+        wait(g, _K[n])
+        rdma(cores[d], T["LAND"][:, BLK * src:BLK * src + BLK], pk[:, BLK * n:BLK * n + BLK], "arr")
+
+    if is_rank:
+        ts("r1", T["qci"][:], T["pco"][:], 15, A.bitwise_and)
+        inc(V.tensor_copy(T["qif"][:], T["qi"][:]), "r1")
+        wait(V, "r1")
+        inc(V.tensor_copy(T["qcf"][:], T["qci"][:]), "r2")
+        ts("r2", T["qc2"][:], T["qci"][:], 2.0, A.mult, 15.0, A.subtract)
+        wait(V, "g6")
+        ts("r3", T["mcu"][:], T["gro"][0:72, :], T["qif"][0:72, :], A.is_ge)
+        ts("r3", T["mcn"][:], T["gro"][0:72, :], T["qif"][0:72, :], A.is_equal)
+        wait(V, "r2")
+        ts("r3", T["rr"][:], T["aro"][:], T["qc2"][:], A.is_equal, -1.0, A.mult)
+        ts("r3", T["pc"][:], T["prow"][:], T["qcf"][:], A.add)
+
+        wait(Y, "exa", "lex")
+        inc(Y.dma_start(T["EXS"][:], T["EXL"][:]), "lexs", 16)
+        wait(V, "lexs")
+        for e in range(EL):
+            ts("r4", T["ohr"][:, 64 * e:64 * e + 64], T["EXS"][:], float(EL * rank + e), A.is_equal)
+        wait(V, "r4")
+        for e in range(EL):
+            inc(V.tensor_reduce(T["cn"][:, e:e + 1], T["ohr"][:, 64 * e:64 * e + 64], AX, A.add), "r5")
+        pc_ = T["psC"]
+        wait(PE, "r0", "r3", "r5")
+        PE.matmul(pc_[:, 0:2], T["mcu"][:], T["cn"][:], True, True)
+        PE.matmul(pc_[:, 2:4], T["mcn"][:], T["cn"][:], True, True)
+        inc(PE.matmul(pc_[0:16, 4:6], T["onf"][:], T["cn"][:], True, True), "p2")
+        wait(V, "p2", "r3")
+        ts("r6", T["wn"][:], pc_[:, 2:4], 128.0, A.subtract)
+        for e in range(EL):
+            ts("r7", T["th9"][:, 16 * e:16 * e + 16], T["pc"][0:16, 16 * e:16 * e + 16], pc_[0:16, 4 + e:5 + e],
+               A.is_ge, -float(ZERO), A.mult)
+        wait(V, "r6")
+        for e in range(EL):
+            ts("r7", T["th"][:, 16 * e:16 * e + 16], T["pc"][:, 16 * e:16 * e + 16], pc_[:, e:e + 1], A.is_ge,
+               T["wn"][:, e:e + 1], A.mult)
+        po = T["psO"]
+        wait(PE, "g6")
+        PE.matmul(po[:, 0:32], T["onb"][:], T["brow"][:], True, False)
+        wait(PE, "r7")
+        PE.matmul(po[:, 0:32], T["rr"][0:16, :], T["th9"][:], False, False)
+        inc(PE.matmul(po[:, 0:32], T["rr"][:], T["th"][:], False, True), "p3")
+        wait(V, "p3")
+        ts("r8", T["yl"][:], po[:, 0:32], T["qcf"][:], A.add, float(ZERO), A.min)
+
+        wait(V, "r8", "pk6", "arr")
+        inc(V.tensor_copy(T["Y0"][:], T["LAND"][:].indirect(T["yl"][:, 0:15])), "yg0")
+        wait(S, "r8", "r0", "pk6", "arr")
+        inc(S.activation(T["Y1"][:], T["LAND"][:].indirect(T["yl"][:, 16:31]), Copy, bias=-0.0), "yg1")
+        wait(Y, "yg0")
+        inc(Y.dma_start(T["y"][:, 0:CAP], T["Y0"][:]), "sty0", 16)
+        wait(S, "yg1")
+        inc(S.dma_start(T["y"][:, CAP:2 * CAP], T["Y1"][:]), "sty1", 16)
+
+    for name in sorted(cnt):
+        if seen.get(name, 0) < cnt[name]:
+            wait(g, name)

@@ -9,39 +9,24 @@ NAG = 3
 MAGIC = 1.5 * 2.0 ** 28
 BIG = 4096.0
 
-SCRATCH = {
-    "E4": ("sbuf", [128, 4], "int32"),
-    "X": ("sbuf", [128, 512], "float32"),
-    "PACK": ("sbuf", [128, 6 * BLK], "float32"),
-    "LAND": ("sbuf", [128, ZERO + 4], "float32"),
-    "Y0": ("sbuf", [128, CAP], "float32"),
-    "Y1": ("sbuf", [128, CAP], "float32"),
-    "EXL": ("dram", [N, 128, 4], "int32"),
-    "EXS": ("sbuf", [72, 64], "int32"),
-    "pco": ("sbuf", [128, 1], "int32"), "ai": ("sbuf", [128, 1], "int32"), "qi": ("sbuf", [128, 1], "int32"),
-    "a16": ("sbuf", [128, 1], "float32"), "a16p": ("sbuf", [128, 1], "float32"), "a64": ("sbuf", [128, 1], "float32"),
-    "kc": ("sbuf", [128, 1], "float32"), "jt": ("sbuf", [128, 4], "float32"),
-    "kap": ("sbuf", [128, 128], "bfloat16"), "kro": ("sbuf", [128, 18], "bfloat16"), "krk": ("sbuf", [1, 72], "bfloat16"),
-    "m15": ("sbuf", [1, 72], "bfloat16"), "aro": ("sbuf", [128, 128], "bfloat16"), "bro": ("sbuf", [128, 72], "bfloat16"),
-    "onb": ("sbuf", [1, 128], "bfloat16"), "msk": ("sbuf", [128, 72], "float32"),
-    "meq": ("sbuf", [128, 128], "bfloat16"), "dia": ("sbuf", [128, 128], "bfloat16"),
-    "mle": ("sbuf", [128, 128], "bfloat16"), "mlt": ("sbuf", [128, 128], "bfloat16"),
-    "e4f": ("sbuf", [128, 4], "float32"), "oh": ("sbuf", [128, 72], "bfloat16"), "sc": ("sbuf", [128, 72], "float32"),
-    "hh": ("sbuf", [128, 4], "float32"), "lo": ("sbuf", [128, 4], "float32"),
-    "bm": ("sbuf", [128, 288], "float16"), "am": ("sbuf", [128, 512], "float16"), "lst": ("sbuf", [128, 72], "uint16"),
-    "onf": ("sbuf", [72, 16], "float32"), "gro": ("sbuf", [128, 128], "bfloat16"), "qif": ("sbuf", [128, 1], "float32"),
-    "mcu": ("sbuf", [72, 128], "float32"), "mcn": ("sbuf", [72, 128], "float32"),
-    "prow": ("sbuf", [128, 32], "float32"), "pc": ("sbuf", [128, 32], "float32"), "brow": ("sbuf", [1, 32], "bfloat16"),
-    "qci": ("sbuf", [128, 1], "int32"), "qcf": ("sbuf", [128, 1], "float32"), "qc2": ("sbuf", [128, 1], "float32"),
-    "rr": ("sbuf", [128, 128], "bfloat16"), "ohr": ("sbuf", [72, 128], "float32"), "cn": ("sbuf", [72, 2], "float32"),
-    "wn": ("sbuf", [128, 2], "float32"), "th": ("sbuf", [128, 32], "bfloat16"), "th9": ("sbuf", [16, 32], "bfloat16"),
-    "yl": ("sbuf", [128, 32], "uint16"),
-    "psP": ("psum", [128, 512], "float32"), "psG": ("psum", [128, 512], "float32"),
-    "psC": ("psum", [128, 512], "float32"), "psO": ("psum", [128, 512], "float32"),
-}
+SCRATCH = {"EXL": ("dram", [N, 128, 4], "int32")}
+for _t, _bufs in {
+    "int32": {"E4": 4, "EXS": (72, 64), "pco": 1, "ai": 1, "qi": 1, "qci": 1},
+    "float32": {"X": 512, "PACK": 3 * BLK, "LAND": ZERO + 4, "Y0": CAP, "Y1": CAP, "a16": 1, "a16p": 1, "a64": 1, "kc": 1, "jt": 4,
+                "msk": 72, "e4f": 4, "sc": 72, "hh": 4, "lo": 4, "onf": (72, 16), "qif": 1, "mcu": (72, 128), "mcn": (72, 128),
+                "prow": 32, "pc": 32, "qcf": 1, "qc2": 1, "ohr": (72, 128), "cn": (72, 2), "wn": 2},
+    "bfloat16": {"kap": 128, "kro": 18, "krk": (1, 72), "m15": (1, 72), "aro": 128, "bro": 72, "onb": (1, 128), "meq": 128,
+                 "dia": 128, "mle": 128, "mlt": 128, "oh": 72, "gro": 128, "brow": (1, 32), "rr": 128, "th": 32, "th9": (16, 32)},
+    "float16": {"bm": 288, "am": 512},
+    "uint16": {"lst": 72, "yl": 32},
+}.items():
+    for _n, _s in _bufs.items():
+        SCRATCH[_n] = ("sbuf", list(_s) if isinstance(_s, tuple) else [128, _s], _t)
+for _n in ("psP", "psG", "psC", "psO"):
+    SCRATCH[_n] = ("psum", [128, 512], "float32")
 _K = ["pk%d" % i for i in range(7)]
 _AB = ["ab%d" % i for i in range(4)]
-SEMAPHORES = (["le4", "lx", "lex", "lexs", "ls", "e4a", "xa", "exa", "arr", "sty0", "sty1", "yg0", "yg1"]
+SEMAPHORES = (["le4", "lx", "lex", "lexs", "ls", "xa", "exa", "arr", "sty0", "sty1", "yg0", "yg1"]
               + ["v%d" % i for i in range(16)] + ["r%d" % i for i in range(10)] + ["g%d" % i for i in range(8)]
               + ["p%d" % i for i in range(4)] + _K + _AB)
 
@@ -52,11 +37,15 @@ def plan(topo, cores):
         far = [d for d in range(N) if topo.rack(topo.host(cores[d])) != topo.rack(topo.host(c))]
         far.sort(key=lambda d: (topo.may_write(c, cores[d]), d))
         ag = far[:NAG]
-        cand = [k for k in range(512) if topo.rack(topo.host(k)) != topo.rack(topo.host(c)) and topo.may_write(c, k)
-                and topo.chip(k) == topo.chip(c) and topo.die(k) != topo.die(c) and k not in cores
-                and all(topo.may_write(k, cores[d]) for d in ag)]
+        here = [d for d in range(N) if d != r and topo.host(cores[d]) == topo.host(c)]
+        he = [d for d in range(N) if d != r and d not in ag and d not in here]
+        agent = [k for k in range(512) if topo.rack(topo.host(k)) != topo.rack(topo.host(c)) and topo.may_write(c, k)
+                 and topo.chip(k) == topo.chip(c) and topo.die(k) != topo.die(c) and k not in cores
+                 and all(topo.may_write(k, cores[d]) for d in ag)]
+        helper = [k for k in range(512) if topo.host(k) == topo.host(c) and topo.chip(k) == topo.chip(c)
+                  and topo.die(k) == topo.die(c) and k not in cores and all(topo.may_write(k, cores[d]) for d in he)]
         rot = lambda ds: sorted(ds, key=lambda d: (d - r) % N)
-        out.append({"agent": cand[0], "direct": rot([d for d in range(N) if d != r and d not in ag]), "via": rot(ag)})
+        out.append({"agent": agent[0], "helper": helper[-1], "direct": rot(here), "via": rot(ag), "near": rot(he)})
     return out
 
 
@@ -64,17 +53,20 @@ def rank_program(g, core, T, topo):
     cores = list(T.cores)
     P = plan(topo, cores)
     rank = T.rank_of(core)
-    agents = {p["agent"]: s for s, p in enumerate(P)}
-    if rank is None and core not in agents:
+    proxies = {}
+    for s, p in enumerate(P):
+        proxies[p["agent"]] = (s, p["via"])
+        proxies[p["helper"]] = (s, p["near"])
+    if rank is None and core not in proxies:
         return
     is_rank = rank is not None
-    src = rank if is_rank else agents[core]
-    dests = P[src]["direct"] if is_rank else P[src]["via"]
+    src, dests = (rank, P[rank]["direct"]) if is_rank else proxies[core]
     outs = [cores[d] for d in dests] + ([P[src]["agent"]] if is_rank else [])
     em = 0xFFFF
     for o in outs:
         em = em & topo.mask(core, o)
     ne = bin(em).count("1")
+    up = topo.mask(core, P[rank]["helper"]) & ~em if is_rank else 0
 
     V, S, PE, Y = g.vector, g.scalar, g.tensor, g.sync
     A = AluOpType
@@ -94,20 +86,19 @@ def rank_program(g, core, T, topo):
     def expect(name, n):
         cnt[name] = cnt.get(name, 0) + n
 
-    def rdma(dst, out_ap, in_ap, sem):
+    def rdma(dst, out_ap, in_ap, sem, mask=em):
         rid, pid = topo.addr(dst, core)
         g.remote_dma(out_ap=out_ap, in_ap=in_ap, remote_sem=T.sem[sem], local_sem=T.sem["ls"], pid=pid, routing_id=rid,
-                     dma_engine_mask=em)
-        expect("ls", ne)
+                     dma_engine_mask=mask)
+        expect("ls", bin(mask).count("1"))
 
-    def send_lists(ds):
-        ids, aps = [], []
+    def spread(ds, ap, sem):
+        ids = []
         for d in ds:
             rid, pid = topo.addr(d, core)
             ids.append(DstId(rid=rid, pnc=pid))
-            aps.append(T["EXL"][src])
-        g.remote_dma_fused([RemoteDMATransfer(dst_ids=ids, dma_engine_mask=em, remote_sem=T.sem["exa"], srcs=[T["EXL"][src]],
-                                              dsts=aps, alu_op=0)], local_sem=T.sem["ls"])
+        g.remote_dma_fused([RemoteDMATransfer(dst_ids=ids, dma_engine_mask=em, remote_sem=T.sem[sem], srcs=[ap],
+                                              dsts=[ap for d in ds], alu_op=0)], local_sem=T.sem["ls"])
         expect("ls", ne)
 
     def iota(name, pattern, base, mult, sem):
@@ -122,22 +113,37 @@ def rank_program(g, core, T, topo):
     if is_rank:
         expect("exa", (N - 1) * ne)
         expect("arr", (N - 1) * ne)
-        inc(Y.dma_start(T["E4"][:], T["ex"][:]), "le4", 16)
-        inc(S.dma_start(T["X"][:], T["x"][:]), "lx", 16)
         inc(Y.dma_start(T["EXL"][rank], T["ex"][:]), "lex", 16)
-        e4sem, xsem = "le4", "lx"
+        inc(S.dma_start(T["X"][:], T["x"][:]), "lx", 16)
+        inc(Y.dma_start(T["E4"][:], T["ex"][:]), "le4", 16)
+        xsem = "lx"
     else:
-        expect("e4a", ne)
         expect("xa", ne)
         expect("exa", ne)
-        e4sem, xsem = "e4a", "xa"
+        xsem = "xa"
+        wait(Y, "exa")
+        inc(Y.dma_start(T["E4"][:], T["EXL"][src]), "le4", 16)
 
     inc(g.iota(T["pco"][:], [[0, 1]], 0, 1), "g0")
     iota("kap", [[1, 16], [16, 8]], 0, 0, "g1")
     iota("kro", [[1, 18]], 0, 0, "g2")
+    if is_rank:
+        ag, he = P[rank]["agent"], P[rank]["helper"]
+        wait(g, "lex")
+        spread([ag, he] + [cores[d] for d in dests], T["EXL"][rank], "exa")
+        wait(g, "lx")
+        rdma(ag, T["X"][:], T["X"][:], "xa")
+        rdma(he, T["X"][:], T["X"][:], "xa", up)
     iota("krk", [[0, 4], [128, 18]], 128, 0, "g3")
     iota("bro", [[32, 72]], int(BIG) + 128, 0, "g4")
     iota("aro", [[0, 8], [2, 16]], -15, 0, "g5")
+    if is_rank:
+        iota("gro", [[1, 8], [0, 16]], 0, 0, "g6")
+        iota("prow", [[0, 2], [16, 16]], 0, 0, "g6")
+        iota("brow", [[64, 2], [16, 16]], 0, 0, "g6")
+    else:
+        wait(g, "exa")
+        spread([cores[d] for d in dests], T["EXL"][src], "exa")
 
     inc(V.memset(T["onb"][:], 1.0), "v0")
     inc(V.memset(T["m15"][:], -15.0), "v0")
@@ -164,22 +170,7 @@ def rank_program(g, core, T, topo):
     ts("v6", T["mle"][:], T["kap"][:], T["a16"][:], A.is_ge, 2.0, A.mult)
     ts("v6", T["mlt"][:], T["kap"][:], T["a16p"][:], A.is_ge, 2.0, A.mult)
 
-    if is_rank:
-        ag = P[rank]["agent"]
-        wait(g, "le4")
-        rdma(ag, T["E4"][:], T["E4"][:], "e4a")
-        wait(g, "lx")
-        rdma(ag, T["X"][:], T["X"][:], "xa")
-        wait(g, "lex")
-        send_lists([ag] + [cores[d] for d in dests])
-        iota("gro", [[1, 8], [0, 16]], 0, 0, "g6")
-        iota("prow", [[0, 2], [16, 16]], 0, 0, "g6")
-        iota("brow", [[64, 2], [16, 16]], 0, 0, "g6")
-    else:
-        wait(g, "exa")
-        send_lists([cores[d] for d in dests])
-
-    wait(V, e4sem)
+    wait(V, "le4")
     inc(V.tensor_copy(T["e4f"][:], T["E4"][:]), "v9")
     wait(V, "v9", "g2")
     for i in range(4):
@@ -233,14 +224,10 @@ def rank_program(g, core, T, topo):
     wait(S, "v14", xsem)
     pk = T["PACK"]
     for n, d in enumerate(dests):
-        o = pk[:, BLK * n:BLK * n + BLK]
-        if is_rank or n < 2:
-            (vget if n % 2 == 0 else sget)(o, off(d), _K[n])
-        else:
-            vget(pk[:, BLK * n:BLK * n + 64], off(d, 0), _K[n])
-            sget(pk[:, BLK * n + 64:BLK * n + 128], off(d, 1), _K[n])
+        vget(pk[:, BLK * n:BLK * n + 64], off(d, 0), _K[n])
+        sget(pk[:, BLK * n + 64:BLK * n + 128], off(d, 1), _K[n])
     if is_rank:
-        sget(T["LAND"][:, BLK * rank:BLK * rank + BLK], off(rank), "pk6")
+        vget(T["LAND"][:, BLK * rank:BLK * rank + BLK], off(rank), "pk6")
     for n, d in enumerate(dests):
         wait(g, _K[n])
         rdma(cores[d], T["LAND"][:, BLK * src:BLK * src + BLK], pk[:, BLK * n:BLK * n + BLK], "arr")

@@ -5,14 +5,16 @@ from concourse.mybir import AluOpType, ActivationFunctionType, AxisListType
 N, EL, CAP = 9, 2, 240
 BLK = 128
 ZERO = N * BLK
-NAG = 3
+NV = 3
 MAGIC = 1.5 * 2.0 ** 28
 BIG = 4096.0
+STEPS = ((0, 1), (1, 2), (2, 3))
 
 SCRATCH = {"EXL": ("dram", [N, 128, 4], "int32")}
 for _t, _bufs in {
     "int32": {"E4": 4, "EXS": (72, 64), "pco": 1, "ai": 1, "qi": 1, "qci": 1},
-    "float32": {"X": 512, "PACK": 3 * BLK, "LAND": ZERO + 4, "Y0": CAP, "Y1": CAP, "a16": 1, "a16p": 1, "a64": 1, "kc": 1, "jt": 4,
+    "float32": {"X": 512, "PA": NV * BLK, "PH": NV * BLK, "PD": 2 * BLK, "LAND": ZERO + 4, "Y0": 2 * CAP,
+                "a16": 1, "a16p": 1, "a64": 1, "kc": 1, "jt": 4, "c32": 72, "c128": (1, 72), "one": 72,
                 "msk": 72, "e4f": 4, "sc": 72, "hh": 4, "lo": 4, "onf": (72, 16), "qif": 1, "mcu": (72, 128), "mcn": (72, 128),
                 "prow": 32, "pc": 32, "qcf": 1, "qc2": 1, "ohr": (72, 128), "cn": (72, 2), "wn": 2},
     "bfloat16": {"kap": 128, "kro": 18, "krk": (1, 72), "m15": (1, 72), "aro": 128, "bro": 72, "onb": (1, 128), "meq": 128,
@@ -24,28 +26,44 @@ for _t, _bufs in {
         SCRATCH[_n] = ("sbuf", list(_s) if isinstance(_s, tuple) else [128, _s], _t)
 for _n in ("psP", "psG", "psC", "psO"):
     SCRATCH[_n] = ("psum", [128, 512], "float32")
-_K = ["pk%d" % i for i in range(7)]
+_K = ["pk%d" % i for i in range(5)]
+_B = ["b%d" % i for i in range(3)]
 _AB = ["ab%d" % i for i in range(4)]
-SEMAPHORES = (["le4", "lx", "lex", "lexs", "ls", "xa", "exa", "arr", "sty0", "sty1", "yg0", "yg1"]
-              + ["v%d" % i for i in range(16)] + ["r%d" % i for i in range(10)] + ["g%d" % i for i in range(8)]
-              + ["p%d" % i for i in range(4)] + _K + _AB)
+SEMAPHORES = (["le4", "lx", "lex", "lexs", "ls", "exa", "arr", "sty", "yg", "own"]
+              + ["v%d" % i for i in range(17)] + ["r%d" % i for i in range(10)] + ["g%d" % i for i in range(8)]
+              + ["p%d" % i for i in range(4)] + _K + _B + _AB)
 
 
 def plan(topo, cores):
-    out = []
+    far = lambda a, b: topo.rack(topo.host(a)) != topo.rack(topo.host(b))
+    place = lambda a: (topo.host(a), topo.chip(a))
+    rot = lambda r, ds: sorted(ds, key=lambda d: (d - r) % N)
+    out, load, used = [], {}, set(cores)
+
+    def carry(c, ds):
+        for d in ds:
+            for port in (("in", place(cores[d]), topo.die(c)), ("out", place(c), topo.die(c))):
+                load[port] = load.get(port, 0) + 1
+
     for r, c in enumerate(cores):
-        far = [d for d in range(N) if topo.rack(topo.host(cores[d])) != topo.rack(topo.host(c))]
-        far.sort(key=lambda d: (topo.may_write(c, cores[d]), d))
-        ag = far[:NAG]
+        fs = sorted((d for d in range(N) if far(cores[d], c)), key=lambda d: (topo.may_write(c, cores[d]), d))
+        ag = fs[:NV]
         here = [d for d in range(N) if d != r and topo.host(cores[d]) == topo.host(c)]
         he = [d for d in range(N) if d != r and d not in ag and d not in here]
-        agent = [k for k in range(512) if topo.rack(topo.host(k)) != topo.rack(topo.host(c)) and topo.may_write(c, k)
-                 and topo.chip(k) == topo.chip(c) and topo.die(k) != topo.die(c) and k not in cores
-                 and all(topo.may_write(k, cores[d]) for d in ag)]
-        helper = [k for k in range(512) if topo.host(k) == topo.host(c) and topo.chip(k) == topo.chip(c)
-                  and topo.die(k) == topo.die(c) and k not in cores and all(topo.may_write(k, cores[d]) for d in he)]
-        rot = lambda ds: sorted(ds, key=lambda d: (d - r) % N)
-        out.append({"agent": agent[0], "helper": helper[-1], "direct": rot(here), "via": rot(ag), "near": rot(he)})
+        out.append({"direct": rot(r, here), "via": rot(r, ag), "near": rot(r, he)})
+        carry(c, here)
+    for kind, ds in (("agent", "via"), ("helper", "near")):
+        for r, c in enumerate(cores):
+            to = out[r][ds]
+            ks = [k for k in range(512) if k not in used and topo.chip(k) == topo.chip(c) and topo.may_write(c, k)
+                  and all(topo.may_write(k, cores[d]) for d in to)
+                  and (far(k, c) if kind == "agent" else topo.host(k) == topo.host(c))]
+            cost = lambda k: (sum(load.get(("in", place(cores[d]), topo.die(k)), 0) for d in to)
+                              + NV * load.get(("out", place(k), topo.die(k)), 0), topo.die(k) != topo.die(c), -k)
+            k = min(ks, key=cost)
+            out[r][kind] = k
+            used.add(k)
+            carry(k, to)
     return out
 
 
@@ -53,20 +71,12 @@ def rank_program(g, core, T, topo):
     cores = list(T.cores)
     P = plan(topo, cores)
     rank = T.rank_of(core)
-    proxies = {}
+    relays = {}
     for s, p in enumerate(P):
-        proxies[p["agent"]] = (s, p["via"])
-        proxies[p["helper"]] = (s, p["near"])
-    if rank is None and core not in proxies:
+        relays[p["agent"]] = (s, p["via"], "PA")
+        relays[p["helper"]] = (s, p["near"], "PH")
+    if rank is None and core not in relays:
         return
-    is_rank = rank is not None
-    src, dests = (rank, P[rank]["direct"]) if is_rank else proxies[core]
-    outs = [cores[d] for d in dests] + ([P[src]["agent"]] if is_rank else [])
-    em = 0xFFFF
-    for o in outs:
-        em = em & topo.mask(core, o)
-    ne = bin(em).count("1")
-    up = topo.mask(core, P[rank]["helper"]) & ~em if is_rank else 0
 
     V, S, PE, Y = g.vector, g.scalar, g.tensor, g.sync
     A = AluOpType
@@ -86,20 +96,58 @@ def rank_program(g, core, T, topo):
     def expect(name, n):
         cnt[name] = cnt.get(name, 0) + n
 
-    def rdma(dst, out_ap, in_ap, sem, mask=em):
-        rid, pid = topo.addr(dst, core)
-        g.remote_dma(out_ap=out_ap, in_ap=in_ap, remote_sem=T.sem[sem], local_sem=T.sem["ls"], pid=pid, routing_id=rid,
-                     dma_engine_mask=mask)
-        expect("ls", bin(mask).count("1"))
+    def finish():
+        for name in sorted(cnt):
+            if seen.get(name, 0) < cnt[name]:
+                wait(g, name)
 
-    def spread(ds, ap, sem):
-        ids = []
+    def ids(ds):
+        res = []
         for d in ds:
             rid, pid = topo.addr(d, core)
-            ids.append(DstId(rid=rid, pnc=pid))
-        g.remote_dma_fused([RemoteDMATransfer(dst_ids=ids, dma_engine_mask=em, remote_sem=T.sem[sem], srcs=[ap],
-                                              dsts=[ap for d in ds], alu_op=0)], local_sem=T.sem["ls"])
-        expect("ls", ne)
+            res.append(DstId(rid=rid, pnc=pid))
+        return res
+
+    def send(*trs):
+        g.remote_dma_fused([RemoteDMATransfer(dst_ids=ids(ds), dma_engine_mask=m, remote_sem=T.sem[sem], srcs=[src],
+                                              dsts=[dst for d in ds], alu_op=0) for ds, dst, src, sem, m in trs],
+                           local_sem=T.sem["ls"])
+        for tr in trs:
+            expect("ls", bin(tr[4]).count("1"))
+
+    def common(ds):
+        m = topo.mask(core, ds[0])
+        for d in ds:
+            m = m & topo.mask(core, d)
+        return m
+
+    def halves(m):
+        bits = [1 << i for i in range(m.bit_length()) if m >> i & 1]
+        return sum(bits[:len(bits) // 2]), sum(bits[len(bits) // 2:])
+
+    if rank is None:
+        src, dests, buf = relays[core]
+        outs = [cores[d] for d in dests]
+        em = common(outs)
+        inm = common([cores[src]]) if False else None
+        ne = bin(em).count("1")
+        expect("exa", ne)
+        wait(g, "exa")
+        send((outs, T["EXL"][src], T["EXL"][src], "exa", em))
+        for n, (a, b) in enumerate(STEPS):
+            expect(_B[n], ne)
+            wait(g, _B[n])
+            for i in range(a, b):
+                send(([outs[i]], T["LAND"][:, BLK * src:BLK * src + BLK], T[buf][:, BLK * i:BLK * i + BLK], "arr", em))
+        finish()
+        return
+
+    me = P[rank]
+    ag, he = me["agent"], me["helper"]
+    outs = [cores[d] for d in me["direct"]]
+    em = common(outs + [ag])
+    up = topo.mask(core, he) & ~em
+    ne = bin(em).count("1")
 
     def iota(name, pattern, base, mult, sem):
         inc(g.iota(T[name][:], pattern, base, mult, allow_small_or_imprecise_dtypes=True), sem)
@@ -110,65 +158,46 @@ def rank_program(g, core, T, topo):
         else:
             inc(V.tensor_scalar(out, in0, s1, s2, op0, op1), sem)
 
-    if is_rank:
-        expect("exa", (N - 1) * ne)
-        expect("arr", (N - 1) * ne)
-        inc(Y.dma_start(T["EXL"][rank], T["ex"][:]), "lex", 16)
-        inc(S.dma_start(T["X"][:], T["x"][:]), "lx", 16)
-        inc(Y.dma_start(T["E4"][:], T["ex"][:]), "le4", 16)
-        xsem = "lx"
-    else:
-        expect("xa", ne)
-        expect("exa", ne)
-        xsem = "xa"
-        wait(Y, "exa")
-        inc(Y.dma_start(T["E4"][:], T["EXL"][src]), "le4", 16)
+    expect("exa", (N - 1) * ne)
+    expect("arr", 2 * NV * ne + len(outs) * (ne // 2))
+    inc(Y.dma_start(T["E4"][:], T["ex"][:]), "le4", 16)
+    inc(S.dma_start(T["EXL"][rank], T["ex"][:]), "lex", 16)
+    inc(Y.dma_start(T["X"][:], T["x"][:]), "lx", 16)
 
     inc(g.iota(T["pco"][:], [[0, 1]], 0, 1), "g0")
     iota("kap", [[1, 16], [16, 8]], 0, 0, "g1")
     iota("kro", [[1, 18]], 0, 0, "g2")
-    if is_rank:
-        ag, he = P[rank]["agent"], P[rank]["helper"]
-        wait(g, "lex")
-        spread([ag, he] + [cores[d] for d in dests], T["EXL"][rank], "exa")
-        wait(g, "lx")
-        rdma(ag, T["X"][:], T["X"][:], "xa")
-        rdma(he, T["X"][:], T["X"][:], "xa", up)
-    iota("krk", [[0, 4], [128, 18]], 128, 0, "g3")
-    iota("bro", [[32, 72]], int(BIG) + 128, 0, "g4")
     iota("aro", [[0, 8], [2, 16]], -15, 0, "g5")
-    if is_rank:
-        iota("gro", [[1, 8], [0, 16]], 0, 0, "g6")
-        iota("prow", [[0, 2], [16, 16]], 0, 0, "g6")
-        iota("brow", [[64, 2], [16, 16]], 0, 0, "g6")
-    else:
-        wait(g, "exa")
-        spread([cores[d] for d in dests], T["EXL"][src], "exa")
+    wait(g, "lex")
+    send(([ag, he] + outs, T["EXL"][rank], T["EXL"][rank], "exa", em))
 
     inc(V.memset(T["onb"][:], 1.0), "v0")
     inc(V.memset(T["m15"][:], -15.0), "v0")
     inc(V.memset(T["msk"][:], 1.0), "v1")
-    if is_rank:
-        inc(V.memset(T["onf"][:], 1.0), "r0")
-        inc(V.memset(T["LAND"][:, ZERO:ZERO + 4], 0.0), "r0")
+    inc(V.memset(T["c128"][:], 128.0), "v7")
+    inc(V.memset(T["one"][:], 1.0), "v7")
+    inc(V.memset(T["c32"][:], 32.0), "v7")
+    wait(V, "v1")
+    inc(V.memset(T["msk"][:, 0:72:18], 0.0), "v3")
     wait(V, "g0")
     ts("v2", T["ai"][:], T["pco"][:], 7, A.bitwise_and)
     ts("v2", T["qi"][:], T["pco"][:], 3, A.arith_shift_right)
-    wait(V, "v1")
-    inc(V.memset(T["msk"][:, 0:72:18], 0.0), "v3")
     wait(V, "v2")
     ts("v4", T["a16"][:], T["ai"][:], 16.0, A.mult)
     ts("v4", T["a16p"][:], T["ai"][:], 16.0, A.mult, 16.0, A.add)
     ts("v4", T["a64"][:], T["ai"][:], 64.0, A.mult)
-    wait(V, "v4")
+    wait(V, "v4", "g1")
     ts("v5", T["kc"][:], T["qi"][:], T["a16"][:], A.add)
-    for i in range(4):
-        ts("v8", T["jt"][:, i:i + 1], T["qi"][:], T["a64"][:], A.add, 16.0 * i, A.add)
-    wait(V, "v5", "g1")
-    ts("v6", T["meq"][:], T["kap"][:], T["kc"][:], A.is_gt, 2.0, A.mult)
-    ts("v6", T["dia"][:], T["kap"][:], T["kc"][:], A.is_equal, BIG, A.mult)
     ts("v6", T["mle"][:], T["kap"][:], T["a16"][:], A.is_ge, 2.0, A.mult)
     ts("v6", T["mlt"][:], T["kap"][:], T["a16p"][:], A.is_ge, 2.0, A.mult)
+    wait(V, "v5")
+    ts("v6", T["meq"][:], T["kap"][:], T["kc"][:], A.is_gt, 2.0, A.mult)
+    ts("v6", T["dia"][:], T["kap"][:], T["kc"][:], A.is_equal, BIG, A.mult)
+    wait(V, "v3", "v7")
+    inc(V.tensor_tensor_scan(T["krk"][:], T["msk"][0:1, :], T["c128"][:], 0.0, A.mult, A.add), "v15")
+    inc(V.tensor_tensor_scan(T["bro"][:], T["one"][:], T["c32"][:], BIG + 96.0, A.mult, A.add), "v16")
+    for i in range(4):
+        ts("v8", T["jt"][:, i:i + 1], T["qi"][:], T["a64"][:], A.add, 16.0 * i, A.add)
 
     wait(V, "le4")
     inc(V.tensor_copy(T["e4f"][:], T["E4"][:]), "v9")
@@ -176,7 +205,7 @@ def rank_program(g, core, T, topo):
     for i in range(4):
         ts("v10", T["oh"][:, 18 * i:18 * i + 18], T["kro"][:], T["e4f"][:, i:i + 1], A.is_equal)
     ps, oh = T["psP"], T["oh"]
-    wait(PE, "v0", "g3")
+    wait(PE, "v0", "v15")
     PE.matmul(ps[:, 0:72], T["onb"][:], T["krk"][:], True, False)
     PE.matmul(ps[:, 0:72], T["onb"][:], T["m15"][:], False, False)
     wait(PE, "v6", "v10")
@@ -186,11 +215,11 @@ def rank_program(g, core, T, topo):
         PE.matmul(ps[:, 0:72 - 18 * n], T["mlt"][:], oh[:, 18 * n:72], False, False)
     PE.matmul(ps[:, 0:72], T["meq"][:], oh[:], False, False)
     inc(PE.matmul(ps[:, 0:72], T["dia"][:], oh[:], False, True), "p0")
-    wait(V, "p0", "v3")
+    wait(V, "p0")
     inc(V.tensor_tensor_scan(T["sc"][:], T["msk"][:], ps[:, 0:72], 0.0, A.mult, A.max), "v11")
     wait(V, "v11")
     ts("v12", T["hh"][:], T["sc"][:, 17:72:18], MAGIC, A.add, MAGIC, A.subtract)
-    wait(V, "v12", "v8", "g4", "g5")
+    wait(V, "v12", "v8", "v16", "g5")
     inc(V.tensor_tensor(T["lo"][:], T["sc"][:, 17:72:18], T["hh"][:], A.subtract), "v13")
 
     def bmat(i):
@@ -211,80 +240,79 @@ def rank_program(g, core, T, topo):
     wait(V, "p1")
     inc(V.tensor_copy(T["lst"][:], pg[:, 0:72]), "v14")
 
-    def off(d, h=None):
-        return T["lst"][:, 8 * d:8 * d + 8] if h is None else T["lst"][:, 8 * d + 4 * h:8 * d + 4 * h + 4]
+    def get(buf, n, d, sem):
+        inc(V.tensor_copy(T[buf][:, BLK * n:BLK * n + 64], T["X"][:].indirect(T["lst"][:, 8 * d:8 * d + 4])), sem)
+        inc(S.activation(T[buf][:, BLK * n + 64:BLK * n + 128], T["X"][:].indirect(T["lst"][:, 8 * d + 4:8 * d + 8]), Copy,
+                         bias=-0.0), sem)
 
-    def vget(out, offs, sem):
-        inc(V.tensor_copy(out, T["X"][:].indirect(offs)), sem)
-
-    def sget(out, offs, sem):
-        inc(S.activation(out, T["X"][:].indirect(offs), Copy, bias=-0.0), sem)
-
-    wait(V, "v14", xsem)
-    wait(S, "v14", xsem)
-    pk = T["PACK"]
-    for n, d in enumerate(dests):
-        vget(pk[:, BLK * n:BLK * n + 64], off(d, 0), _K[n])
-        sget(pk[:, BLK * n + 64:BLK * n + 128], off(d, 1), _K[n])
-    if is_rank:
-        vget(T["LAND"][:, BLK * rank:BLK * rank + BLK], off(rank), "pk6")
-    for n, d in enumerate(dests):
+    wait(V, "v14", "lx")
+    wait(S, "v14", "lx")
+    for n, (a, b) in enumerate(STEPS):
+        for i in range(a, b):
+            get("PA", i, me["via"][i], _K[n])
+            get("PH", i, me["near"][i], _K[n])
         wait(g, _K[n])
-        rdma(cores[d], T["LAND"][:, BLK * src:BLK * src + BLK], pk[:, BLK * n:BLK * n + BLK], "arr")
+        pa, ph = T["PA"][:, BLK * a:BLK * b], T["PH"][:, BLK * a:BLK * b]
+        send(([ag], pa, pa, _B[n], em), ([he], ph, ph, _B[n], up))
+    for n, d in enumerate(me["direct"]):
+        get("PD", n, d, _K[4])
+    wait(g, _K[4])
+    here = T["LAND"][:, BLK * rank:BLK * rank + BLK]
+    send(*[([o], here, T["PD"][:, BLK * n:BLK * n + BLK], "arr", m) for n, (o, m) in enumerate(zip(outs, halves(em)))])
+    get("LAND", rank, rank, "own")
 
-    if is_rank:
-        ts("r1", T["qci"][:], T["pco"][:], 15, A.bitwise_and)
-        inc(V.tensor_copy(T["qif"][:], T["qi"][:]), "r1")
-        wait(V, "r1")
-        inc(V.tensor_copy(T["qcf"][:], T["qci"][:]), "r2")
-        ts("r2", T["qc2"][:], T["qci"][:], 2.0, A.mult, 15.0, A.subtract)
-        wait(V, "g6")
-        ts("r3", T["mcu"][:], T["gro"][0:72, :], T["qif"][0:72, :], A.is_ge)
-        ts("r3", T["mcn"][:], T["gro"][0:72, :], T["qif"][0:72, :], A.is_equal)
-        wait(V, "r2")
-        ts("r3", T["rr"][:], T["aro"][:], T["qc2"][:], A.is_equal, -1.0, A.mult)
-        ts("r3", T["pc"][:], T["prow"][:], T["qcf"][:], A.add)
+    iota("gro", [[1, 8], [0, 16]], 0, 0, "g6")
+    iota("prow", [[0, 2], [16, 16]], 0, 0, "g6")
+    iota("brow", [[64, 2], [16, 16]], 0, 0, "g6")
+    inc(V.memset(T["onf"][:], 1.0), "r0")
+    inc(V.memset(T["LAND"][:, ZERO:ZERO + 4], 0.0), "r0")
+    ts("r1", T["qci"][:], T["pco"][:], 15, A.bitwise_and)
+    inc(V.tensor_copy(T["qif"][:], T["qi"][:]), "r1")
+    wait(V, "r1")
+    inc(V.tensor_copy(T["qcf"][:], T["qci"][:]), "r2")
+    ts("r2", T["qc2"][:], T["qci"][:], 2.0, A.mult, 15.0, A.subtract)
+    wait(V, "g6")
+    ts("r3", T["mcu"][:], T["gro"][0:72, :], T["qif"][0:72, :], A.is_ge)
+    ts("r3", T["mcn"][:], T["gro"][0:72, :], T["qif"][0:72, :], A.is_equal)
+    wait(V, "r2")
+    ts("r3", T["rr"][:], T["aro"][:], T["qc2"][:], A.is_equal, -1.0, A.mult)
+    ts("r3", T["pc"][:], T["prow"][:], T["qcf"][:], A.add)
 
-        wait(Y, "exa", "lex")
-        inc(Y.dma_start(T["EXS"][:], T["EXL"][:]), "lexs", 16)
-        wait(V, "lexs")
-        for e in range(EL):
-            ts("r4", T["ohr"][:, 64 * e:64 * e + 64], T["EXS"][:], float(EL * rank + e), A.is_equal)
-        wait(V, "r4")
-        for e in range(EL):
-            inc(V.tensor_reduce(T["cn"][:, e:e + 1], T["ohr"][:, 64 * e:64 * e + 64], AX, A.add), "r5")
-        pc_ = T["psC"]
-        wait(PE, "r0", "r3", "r5")
-        PE.matmul(pc_[:, 0:2], T["mcu"][:], T["cn"][:], True, True)
-        PE.matmul(pc_[:, 2:4], T["mcn"][:], T["cn"][:], True, True)
-        inc(PE.matmul(pc_[0:16, 4:6], T["onf"][:], T["cn"][:], True, True), "p2")
-        wait(V, "p2", "r3")
-        ts("r6", T["wn"][:], pc_[:, 2:4], 128.0, A.subtract)
-        for e in range(EL):
-            ts("r7", T["th9"][:, 16 * e:16 * e + 16], T["pc"][0:16, 16 * e:16 * e + 16], pc_[0:16, 4 + e:5 + e],
-               A.is_ge, -float(ZERO), A.mult)
-        wait(V, "r6")
-        for e in range(EL):
-            ts("r7", T["th"][:, 16 * e:16 * e + 16], T["pc"][:, 16 * e:16 * e + 16], pc_[:, e:e + 1], A.is_ge,
-               T["wn"][:, e:e + 1], A.mult)
-        po = T["psO"]
-        wait(PE, "g6")
-        PE.matmul(po[:, 0:32], T["onb"][:], T["brow"][:], True, False)
-        wait(PE, "r7")
-        PE.matmul(po[:, 0:32], T["rr"][0:16, :], T["th9"][:], False, False)
-        inc(PE.matmul(po[:, 0:32], T["rr"][:], T["th"][:], False, True), "p3")
-        wait(V, "p3")
-        ts("r8", T["yl"][:], po[:, 0:32], T["qcf"][:], A.add, float(ZERO), A.min)
+    wait(Y, "exa", "lex")
+    inc(Y.dma_start(T["EXS"][:], T["EXL"][:]), "lexs", 16)
+    wait(V, "lexs")
+    for e in range(EL):
+        ts("r4", T["ohr"][:, 64 * e:64 * e + 64], T["EXS"][:], float(EL * rank + e), A.is_equal)
+    wait(V, "r4")
+    for e in range(EL):
+        inc(V.tensor_reduce(T["cn"][:, e:e + 1], T["ohr"][:, 64 * e:64 * e + 64], AX, A.add), "r5")
+    pc_ = T["psC"]
+    wait(PE, "r0", "r3", "r5")
+    PE.matmul(pc_[:, 0:2], T["mcu"][:], T["cn"][:], True, True)
+    PE.matmul(pc_[:, 2:4], T["mcn"][:], T["cn"][:], True, True)
+    inc(PE.matmul(pc_[0:16, 4:6], T["onf"][:], T["cn"][:], True, True), "p2")
+    wait(V, "p2", "r3")
+    ts("r6", T["wn"][:], pc_[:, 2:4], 128.0, A.subtract)
+    for e in range(EL):
+        ts("r7", T["th9"][:, 16 * e:16 * e + 16], T["pc"][0:16, 16 * e:16 * e + 16], pc_[0:16, 4 + e:5 + e],
+           A.is_ge, -float(ZERO), A.mult)
+    wait(V, "r6")
+    for e in range(EL):
+        ts("r7", T["th"][:, 16 * e:16 * e + 16], T["pc"][:, 16 * e:16 * e + 16], pc_[:, e:e + 1], A.is_ge,
+           T["wn"][:, e:e + 1], A.mult)
+    po = T["psO"]
+    wait(PE, "g6")
+    PE.matmul(po[:, 0:32], T["onb"][:], T["brow"][:], True, False)
+    wait(PE, "r7")
+    PE.matmul(po[:, 0:32], T["rr"][0:16, :], T["th9"][:], False, False)
+    inc(PE.matmul(po[:, 0:32], T["rr"][:], T["th"][:], False, True), "p3")
+    wait(V, "p3")
+    ts("r8", T["yl"][:], po[:, 0:32], T["qcf"][:], A.add, float(ZERO), A.min)
 
-        wait(V, "r8", "pk6", "arr")
-        inc(V.tensor_copy(T["Y0"][:], T["LAND"][:].indirect(T["yl"][:, 0:15])), "yg0")
-        wait(S, "r8", "r0", "pk6", "arr")
-        inc(S.activation(T["Y1"][:], T["LAND"][:].indirect(T["yl"][:, 16:31]), Copy, bias=-0.0), "yg1")
-        wait(Y, "yg0")
-        inc(Y.dma_start(T["y"][:, 0:CAP], T["Y0"][:]), "sty0", 16)
-        wait(S, "yg1")
-        inc(S.dma_start(T["y"][:, CAP:2 * CAP], T["Y1"][:]), "sty1", 16)
-
-    for name in sorted(cnt):
-        if seen.get(name, 0) < cnt[name]:
-            wait(g, name)
+    wait(V, "r8", "own", "arr")
+    inc(V.tensor_copy(T["Y0"][:, 0:CAP], T["LAND"][:].indirect(T["yl"][:, 0:15])), "yg")
+    wait(S, "r8", "r0", "own", "arr")
+    inc(S.activation(T["Y0"][:, CAP:2 * CAP], T["LAND"][:].indirect(T["yl"][:, 16:31]), Copy, bias=-0.0), "yg")
+    wait(Y, "yg")
+    inc(Y.dma_start(T["y"][:], T["Y0"][:]), "sty", 16)
+    finish()

@@ -8,15 +8,15 @@ ZERO = N * BLK
 NV = 3
 MAGIC = 1.5 * 2.0 ** 28
 BIG = 4096.0
-STEPS = ((0, 1), (1, 2), (2, 3))
+KINDS = (("agent", "via"), ("helper", "near"))
 
 SCRATCH = {"EXL": ("dram", [N, 128, 4], "int32")}
 for _t, _bufs in {
     "int32": {"E4": 4, "EXS": (72, 64), "pco": 1, "ai": 1, "qi": 1, "qci": 1},
     "float32": {"X": 512, "PA": NV * BLK, "PH": NV * BLK, "PD": 2 * BLK, "LAND": ZERO + 4, "Y0": 2 * CAP,
-                "a16": 1, "a16p": 1, "a64": 1, "kc": 1, "jt": 4, "c32": 72, "c128": (1, 72), "one": 72,
-                "msk": 72, "e4f": 4, "sc": 72, "hh": 4, "lo": 4, "onf": (72, 16), "qif": 1, "mcu": (72, 128), "mcn": (72, 128),
-                "prow": 32, "pc": 32, "qcf": 1, "qc2": 1, "ohr": (72, 128), "cn": (72, 2), "wn": 2},
+                "a16": 1, "a16p": 1, "a64": 1, "kc": 1, "jt": 4, "c32": 72, "c128": (1, 72), "on1": (1, 128), "m128": (1, 2),
+                "msk": 72, "e4f": 4, "sc": 72, "hh": 4, "onf": (72, 16), "qif": 1, "mcu": (72, 128), "mcn": (72, 128),
+                "prow": 32, "pc": 32, "qcf": 1, "qc2": 1, "ohr": (72, 128), "cn": (72, 2)},
     "bfloat16": {"kap": 128, "kro": 18, "krk": (1, 72), "m15": (1, 72), "aro": 128, "bro": 72, "onb": (1, 128), "meq": 128,
                  "dia": 128, "mle": 128, "mlt": 128, "oh": 72, "gro": 128, "brow": (1, 32), "rr": 128, "th": 32, "th9": (16, 32)},
     "float16": {"bm": 288, "am": 512},
@@ -24,46 +24,75 @@ for _t, _bufs in {
 }.items():
     for _n, _s in _bufs.items():
         SCRATCH[_n] = ("sbuf", list(_s) if isinstance(_s, tuple) else [128, _s], _t)
-for _n in ("psP", "psG", "psC", "psO"):
+for _n in ("psP", "psG", "psC", "psW", "psO"):
     SCRATCH[_n] = ("psum", [128, 512], "float32")
-_K = ["pk%d" % i for i in range(5)]
-_B = ["b%d" % i for i in range(3)]
+_K = ["pk%d" % i for i in range(NV + 1)]
+_B = ["b%d" % i for i in range(NV)]
 _AB = ["ab%d" % i for i in range(4)]
 SEMAPHORES = (["le4", "lx", "lex", "lexs", "ls", "exa", "arr", "sty", "yg", "own"]
-              + ["v%d" % i for i in range(17)] + ["r%d" % i for i in range(10)] + ["g%d" % i for i in range(8)]
+              + ["v%d" % i for i in range(17)] + ["r%d" % i for i in range(9)] + ["g%d" % i for i in range(8)]
               + ["p%d" % i for i in range(4)] + _K + _B + _AB)
+_PLANS = {}
 
 
 def plan(topo, cores):
+    if "plan" in _PLANS:
+        return _PLANS["plan"]
     far = lambda a, b: topo.rack(topo.host(a)) != topo.rack(topo.host(b))
-    place = lambda a: (topo.host(a), topo.chip(a))
-    rot = lambda r, ds: sorted(ds, key=lambda d: (d - r) % N)
-    out, load, used = [], {}, set(cores)
+    hosts = sorted(set(topo.host(c) for c in cores))
+    nk, nh = len(KINDS), len(hosts)
 
-    def carry(c, ds):
-        for d in ds:
-            for port in (("in", place(cores[d]), topo.die(c)), ("out", place(c), topo.die(c))):
-                load[port] = load.get(port, 0) + 1
+    def ports(k, o):
+        hk, ho, ck, co, die = topo.host(k), topo.host(o), topo.chip(k), topo.chip(o), topo.die(k)
+        if ck == co and (hk == ho or far(k, o)):
+            return (), ()
+        if not far(k, o):
+            w = (("out", hk, ck, die), ("in", ho, co, die))
+            return w, w
+        return (("out", ho, ck, die), ("in", ho, co, die)), (("out", hk, ck, die), ("in", hk, co, die))
 
+    serve, cand, use = [], {}, {}
     for r, c in enumerate(cores):
         fs = sorted((d for d in range(N) if far(cores[d], c)), key=lambda d: (topo.may_write(c, cores[d]), d))
-        ag = fs[:NV]
+        via = sorted(fs[:NV])
         here = [d for d in range(N) if d != r and topo.host(cores[d]) == topo.host(c)]
-        he = [d for d in range(N) if d != r and d not in ag and d not in here]
-        out.append({"direct": rot(r, here), "via": rot(r, ag), "near": rot(r, he)})
-        carry(c, here)
-    for kind, ds in (("agent", "via"), ("helper", "near")):
+        near = [d for d in range(N) if d != r and d not in via and d not in here]
+        turn = lambda ds: [ds[(i + r) % len(ds)] for i in range(len(ds))]
+        serve.append({"via": turn(via), "near": turn(near), "here": sorted(here, key=lambda d: (d - r) % N)})
+        use[r] = [ports(c, cores[d]) for d in here]
+        for kind, ds in KINDS:
+            for k in range(512):
+                if (topo.chip(k) == topo.chip(c) and k not in cores and topo.may_write(c, k)
+                        and all(topo.may_write(k, cores[d]) for d in serve[r][ds])
+                        and (far(k, c) if kind == "agent" else topo.host(k) == topo.host(c))):
+                    cand.setdefault((r, kind, int(topo.die(k) != topo.die(c))), []).append(k)
+            for o in (0, 1):
+                use[r, kind, o] = [ports(cand[r, kind, o][0], cores[d]) for d in serve[r][ds]]
+    best = None
+    for pick in np.ndindex(*([2] * (nk * nh))):
+        loads = ({}, {})
         for r, c in enumerate(cores):
-            to = out[r][ds]
-            ks = [k for k in range(512) if k not in used and topo.chip(k) == topo.chip(c) and topo.may_write(c, k)
-                  and all(topo.may_write(k, cores[d]) for d in to)
-                  and (far(k, c) if kind == "agent" else topo.host(k) == topo.host(c))]
-            cost = lambda k: (sum(load.get(("in", place(cores[d]), topo.die(k)), 0) for d in to)
-                              + NV * load.get(("out", place(k), topo.die(k)), 0), topo.die(k) != topo.die(c), -k)
-            k = min(ks, key=cost)
-            out[r][kind] = k
-            used.add(k)
-            carry(k, to)
+            ws = list(use[r])
+            for i in range(nk):
+                ws += use[r, KINDS[i][0], pick[i * nh + hosts.index(topo.host(c))]]
+            for w in ws:
+                for load, way in zip(loads, w):
+                    for e in way:
+                        load[e] = load.get(e, 0) + 1
+        every = [v for load in loads for v in load.values()]
+        cost = (max(every), sum(pick[nh:]), sum(v * v for v in every))
+        if best is None or cost < best[0]:
+            best = (cost, pick)
+    used, out = set(), []
+    for r, c in enumerate(cores):
+        p = dict(serve[r])
+        for i in range(nk):
+            kind = KINDS[i][0]
+            ks = [k for k in cand[r, kind, best[1][i * nh + hosts.index(topo.host(c))]] if k not in used]
+            p[kind] = ks[-1] if kind == "helper" else ks[0]
+            used.add(p[kind])
+        out.append(p)
+    _PLANS["plan"] = out
     return out
 
 
@@ -73,8 +102,8 @@ def rank_program(g, core, T, topo):
     rank = T.rank_of(core)
     relays = {}
     for s, p in enumerate(P):
-        relays[p["agent"]] = (s, p["via"], "PA")
-        relays[p["helper"]] = (s, p["near"], "PH")
+        relays[p["agent"]] = (s, p["via"], p["via"], "PA")
+        relays[p["helper"]] = (s, p["near"], p["near"] + p["here"], "PH")
     if rank is None and core not in relays:
         return
 
@@ -108,46 +137,47 @@ def rank_program(g, core, T, topo):
             res.append(DstId(rid=rid, pnc=pid))
         return res
 
-    def send(*trs):
-        g.remote_dma_fused([RemoteDMATransfer(dst_ids=ids(ds), dma_engine_mask=m, remote_sem=T.sem[sem], srcs=[src],
-                                              dsts=[dst for d in ds], alu_op=0) for ds, dst, src, sem, m in trs],
-                           local_sem=T.sem["ls"])
-        for tr in trs:
-            expect("ls", bin(tr[4]).count("1"))
-
-    def common(ds):
-        m = topo.mask(core, ds[0])
-        for d in ds:
-            m = m & topo.mask(core, d)
-        return m
+    def size(m):
+        return bin(m).count("1")
 
     def halves(m):
         bits = [1 << i for i in range(m.bit_length()) if m >> i & 1]
         return sum(bits[:len(bits) // 2]), sum(bits[len(bits) // 2:])
 
+    def send(*trs):
+        g.remote_dma_fused([RemoteDMATransfer(dst_ids=ids(ds), dma_engine_mask=m, remote_sem=T.sem[sem], srcs=[src],
+                                              dsts=[dst for d in ds], alu_op=0) for ds, dst, src, sem, m in trs],
+                           local_sem=T.sem["ls"])
+        for tr in trs:
+            expect("ls", size(tr[4]))
+
+    def common(c, ds):
+        m = topo.mask(c, ds[0])
+        for d in ds:
+            m = m & topo.mask(c, d)
+        return m
+
+    def masks(s):
+        m = common(cores[s], [P[s]["agent"]] + [cores[d] for d in P[s]["here"]])
+        return m, topo.mask(cores[s], P[s]["helper"]) & ~m
+
     if rank is None:
-        src, dests, buf = relays[core]
-        outs = [cores[d] for d in dests]
-        em = common(outs)
-        inm = common([cores[src]]) if False else None
-        ne = bin(em).count("1")
-        expect("exa", ne)
+        src, dests, readers, buf = relays[core]
+        em = common(core, [cores[d] for d in readers])
+        leave, stay = masks(src)
+        expect("exa", size(halves(leave)[0]))
         wait(g, "exa")
-        send((outs, T["EXL"][src], T["EXL"][src], "exa", em))
-        for n, (a, b) in enumerate(STEPS):
-            expect(_B[n], ne)
+        send(([cores[d] for d in readers], T["EXL"][src], T["EXL"][src], "exa", em))
+        for n, d in enumerate(dests):
+            expect(_B[n], size(leave if buf == "PA" else stay))
             wait(g, _B[n])
-            for i in range(a, b):
-                send(([outs[i]], T["LAND"][:, BLK * src:BLK * src + BLK], T[buf][:, BLK * i:BLK * i + BLK], "arr", em))
+            send(([cores[d]], T["LAND"][:, BLK * src:BLK * src + BLK], T[buf][:, BLK * n:BLK * n + BLK], "arr", em))
         finish()
         return
 
     me = P[rank]
     ag, he = me["agent"], me["helper"]
-    outs = [cores[d] for d in me["direct"]]
-    em = common(outs + [ag])
-    up = topo.mask(core, he) & ~em
-    ne = bin(em).count("1")
+    leave, stay = masks(rank)
 
     def iota(name, pattern, base, mult, sem):
         inc(g.iota(T[name][:], pattern, base, mult, allow_small_or_imprecise_dtypes=True), sem)
@@ -158,8 +188,16 @@ def rank_program(g, core, T, topo):
         else:
             inc(V.tensor_scalar(out, in0, s1, s2, op0, op1), sem)
 
-    expect("exa", (N - 1) * ne)
-    expect("arr", 2 * NV * ne + len(outs) * (ne // 2))
+    for k in relays:
+        s, dests, readers, buf = relays[k]
+        n = size(common(k, [cores[d] for d in readers]))
+        if rank in readers:
+            expect("exa", n)
+        if rank in dests:
+            expect("arr", n)
+    for s in range(N):
+        if rank in P[s]["here"]:
+            expect("arr", size(halves(masks(s)[0])[0]))
     inc(Y.dma_start(T["E4"][:], T["ex"][:]), "le4", 16)
     inc(S.dma_start(T["EXL"][rank], T["ex"][:]), "lex", 16)
     inc(Y.dma_start(T["X"][:], T["x"][:]), "lx", 16)
@@ -169,23 +207,24 @@ def rank_program(g, core, T, topo):
     iota("kro", [[1, 18]], 0, 0, "g2")
     iota("aro", [[0, 8], [2, 16]], -15, 0, "g5")
     wait(g, "lex")
-    send(([ag, he] + outs, T["EXL"][rank], T["EXL"][rank], "exa", em))
+    send(([ag, he], T["EXL"][rank], T["EXL"][rank], "exa", halves(leave)[0]))
 
-    inc(V.memset(T["onb"][:], 1.0), "v0")
-    inc(V.memset(T["m15"][:], -15.0), "v0")
     inc(V.memset(T["msk"][:], 1.0), "v1")
     inc(V.memset(T["c128"][:], 128.0), "v7")
-    inc(V.memset(T["one"][:], 1.0), "v7")
-    inc(V.memset(T["c32"][:], 32.0), "v7")
+    inc(V.memset(T["onb"][:], 1.0), "v0")
+    inc(V.memset(T["m15"][:], -15.0), "v0")
     wait(V, "v1")
     inc(V.memset(T["msk"][:, 0:72:18], 0.0), "v3")
     wait(V, "g0")
     ts("v2", T["ai"][:], T["pco"][:], 7, A.bitwise_and)
     ts("v2", T["qi"][:], T["pco"][:], 3, A.arith_shift_right)
+    inc(V.memset(T["c32"][:], 32.0), "v7")
     wait(V, "v2")
     ts("v4", T["a16"][:], T["ai"][:], 16.0, A.mult)
     ts("v4", T["a16p"][:], T["ai"][:], 16.0, A.mult, 16.0, A.add)
     ts("v4", T["a64"][:], T["ai"][:], 64.0, A.mult)
+    wait(V, "v3", "v7")
+    inc(V.tensor_tensor_scan(T["krk"][:], T["msk"][0:1, :], T["c128"][:], 0.0, A.mult, A.add), "v15")
     wait(V, "v4", "g1")
     ts("v5", T["kc"][:], T["qi"][:], T["a16"][:], A.add)
     ts("v6", T["mle"][:], T["kap"][:], T["a16"][:], A.is_ge, 2.0, A.mult)
@@ -193,17 +232,15 @@ def rank_program(g, core, T, topo):
     wait(V, "v5")
     ts("v6", T["meq"][:], T["kap"][:], T["kc"][:], A.is_gt, 2.0, A.mult)
     ts("v6", T["dia"][:], T["kap"][:], T["kc"][:], A.is_equal, BIG, A.mult)
-    wait(V, "v3", "v7")
-    inc(V.tensor_tensor_scan(T["krk"][:], T["msk"][0:1, :], T["c128"][:], 0.0, A.mult, A.add), "v15")
-    inc(V.tensor_tensor_scan(T["bro"][:], T["one"][:], T["c32"][:], BIG + 96.0, A.mult, A.add), "v16")
-    for i in range(4):
-        ts("v8", T["jt"][:, i:i + 1], T["qi"][:], T["a64"][:], A.add, 16.0 * i, A.add)
 
     wait(V, "le4")
     inc(V.tensor_copy(T["e4f"][:], T["E4"][:]), "v9")
     wait(V, "v9", "g2")
     for i in range(4):
         ts("v10", T["oh"][:, 18 * i:18 * i + 18], T["kro"][:], T["e4f"][:, i:i + 1], A.is_equal)
+    inc(V.tensor_tensor_scan(T["bro"][:], T["c32"][:], T["c32"][:], BIG + 96.0, A.add, A.max), "v16")
+    for i in range(4):
+        ts("v8", T["jt"][:, i:i + 1], T["qi"][:], T["a64"][:], A.add, 16.0 * i, A.add)
     ps, oh = T["psP"], T["oh"]
     wait(PE, "v0", "v15")
     PE.matmul(ps[:, 0:72], T["onb"][:], T["krk"][:], True, False)
@@ -220,18 +257,10 @@ def rank_program(g, core, T, topo):
     wait(V, "v11")
     ts("v12", T["hh"][:], T["sc"][:, 17:72:18], MAGIC, A.add, MAGIC, A.subtract)
     wait(V, "v12", "v8", "v16", "g5")
-    inc(V.tensor_tensor(T["lo"][:], T["sc"][:, 17:72:18], T["hh"][:], A.subtract), "v13")
-
-    def bmat(i):
-        ts(_AB[i], T["bm"][:, 72 * i:72 * i + 72], T["bro"][:], T["hh"][:, i:i + 1], A.is_equal, T["jt"][:, i:i + 1], A.mult)
-
-    bmat(0)
-    bmat(1)
-    wait(V, "v13")
     for i in range(4):
-        ts(_AB[i], T["am"][:, 128 * i:128 * i + 128], T["aro"][:], T["lo"][:, i:i + 1], A.is_equal)
-        if i + 2 < 4:
-            bmat(i + 2)
+        ts(_AB[i], T["am"][:, 128 * i:128 * i + 128], T["aro"][:], T["hh"][:, i:i + 1], A.add,
+           T["sc"][:, 17 + 18 * i:18 + 18 * i], A.is_equal)
+        ts(_AB[i], T["bm"][:, 72 * i:72 * i + 72], T["bro"][:], T["hh"][:, i:i + 1], A.is_equal, T["jt"][:, i:i + 1], A.mult)
     pg = T["psG"]
     for i in range(4):
         wait(PE, _AB[i])
@@ -240,31 +269,36 @@ def rank_program(g, core, T, topo):
     wait(V, "p1")
     inc(V.tensor_copy(T["lst"][:], pg[:, 0:72]), "v14")
 
-    def get(buf, n, d, sem):
-        inc(V.tensor_copy(T[buf][:, BLK * n:BLK * n + 64], T["X"][:].indirect(T["lst"][:, 8 * d:8 * d + 4])), sem)
-        inc(S.activation(T[buf][:, BLK * n + 64:BLK * n + 128], T["X"][:].indirect(T["lst"][:, 8 * d + 4:8 * d + 8]), Copy,
-                         bias=-0.0), sem)
+    def vget(out, d, sem):
+        inc(V.tensor_copy(out, T["X"][:].indirect(T["lst"][:, 8 * d:8 * d + 8])), sem)
+
+    def sget(out, d, sem):
+        inc(S.activation(out, T["X"][:].indirect(T["lst"][:, 8 * d:8 * d + 8]), Copy, bias=-0.0), sem)
+
+    def block(buf, n):
+        return T[buf][:, BLK * n:BLK * n + BLK]
 
     wait(V, "v14", "lx")
     wait(S, "v14", "lx")
-    for n, (a, b) in enumerate(STEPS):
-        for i in range(a, b):
-            get("PA", i, me["via"][i], _K[n])
-            get("PH", i, me["near"][i], _K[n])
+    for n in range(NV):
+        pa, ph = block("PA", n), block("PH", n)
+        vget(pa, me["via"][n], _K[n])
+        sget(ph, me["near"][n], _K[n])
         wait(g, _K[n])
-        pa, ph = T["PA"][:, BLK * a:BLK * b], T["PH"][:, BLK * a:BLK * b]
-        send(([ag], pa, pa, _B[n], em), ([he], ph, ph, _B[n], up))
-    for n, d in enumerate(me["direct"]):
-        get("PD", n, d, _K[4])
-    wait(g, _K[4])
-    here = T["LAND"][:, BLK * rank:BLK * rank + BLK]
-    send(*[([o], here, T["PD"][:, BLK * n:BLK * n + BLK], "arr", m) for n, (o, m) in enumerate(zip(outs, halves(em)))])
-    get("LAND", rank, rank, "own")
+        send(([ag], pa, pa, _B[n], leave), ([he], ph, ph, _B[n], stay))
+    for n, get in enumerate((vget, sget)):
+        get(block("PD", n), me["here"][n], _K[NV])
+    wait(g, _K[NV])
+    own = block("LAND", rank)
+    send(*[([cores[d]], own, block("PD", n), "arr", m) for n, (d, m) in enumerate(zip(me["here"], halves(leave)))])
+    vget(own, rank, "own")
 
     iota("gro", [[1, 8], [0, 16]], 0, 0, "g6")
     iota("prow", [[0, 2], [16, 16]], 0, 0, "g6")
     iota("brow", [[64, 2], [16, 16]], 0, 0, "g6")
     inc(V.memset(T["onf"][:], 1.0), "r0")
+    inc(V.memset(T["on1"][:], 1.0), "r0")
+    inc(V.memset(T["m128"][:], -128.0), "r0")
     inc(V.memset(T["LAND"][:, ZERO:ZERO + 4], 0.0), "r0")
     ts("r1", T["qci"][:], T["pco"][:], 15, A.bitwise_and)
     inc(V.tensor_copy(T["qif"][:], T["qi"][:]), "r1")
@@ -286,23 +320,21 @@ def rank_program(g, core, T, topo):
     wait(V, "r4")
     for e in range(EL):
         inc(V.tensor_reduce(T["cn"][:, e:e + 1], T["ohr"][:, 64 * e:64 * e + 64], AX, A.add), "r5")
-    pc_ = T["psC"]
-    wait(PE, "r0", "r3", "r5")
+    pc_, pw, po = T["psC"], T["psW"], T["psO"]
+    wait(PE, "g6", "r0")
+    PE.matmul(po[:, 0:32], T["onb"][:], T["brow"][:], True, False)
+    PE.matmul(pw[:, 0:2], T["on1"][:], T["m128"][:], True, False)
+    wait(PE, "r3", "r5")
+    PE.matmul(pw[:, 0:2], T["mcn"][:], T["cn"][:], False, True)
     PE.matmul(pc_[:, 0:2], T["mcu"][:], T["cn"][:], True, True)
-    PE.matmul(pc_[:, 2:4], T["mcn"][:], T["cn"][:], True, True)
-    inc(PE.matmul(pc_[0:16, 4:6], T["onf"][:], T["cn"][:], True, True), "p2")
+    inc(PE.matmul(pc_[0:16, 2:4], T["onf"][:], T["cn"][:], True, True), "p2")
     wait(V, "p2", "r3")
-    ts("r6", T["wn"][:], pc_[:, 2:4], 128.0, A.subtract)
     for e in range(EL):
-        ts("r7", T["th9"][:, 16 * e:16 * e + 16], T["pc"][0:16, 16 * e:16 * e + 16], pc_[0:16, 4 + e:5 + e],
+        ts("r7", T["th9"][:, 16 * e:16 * e + 16], T["pc"][0:16, 16 * e:16 * e + 16], pc_[0:16, 2 + e:3 + e],
            A.is_ge, -float(ZERO), A.mult)
-    wait(V, "r6")
     for e in range(EL):
         ts("r7", T["th"][:, 16 * e:16 * e + 16], T["pc"][:, 16 * e:16 * e + 16], pc_[:, e:e + 1], A.is_ge,
-           T["wn"][:, e:e + 1], A.mult)
-    po = T["psO"]
-    wait(PE, "g6")
-    PE.matmul(po[:, 0:32], T["onb"][:], T["brow"][:], True, False)
+           pw[:, e:e + 1], A.mult)
     wait(PE, "r7")
     PE.matmul(po[:, 0:32], T["rr"][0:16, :], T["th9"][:], False, False)
     inc(PE.matmul(po[:, 0:32], T["rr"][:], T["th"][:], False, True), "p3")

@@ -8,12 +8,13 @@ ZERO = N * BLK
 NV = 3
 MAGIC = 1.5 * 2.0 ** 28
 BIG = 4096.0
-KINDS = (("agent", "via"), ("helper", "near"))
+WORK = {"rank": (("V0", "h0"), ("V1", "n2"), ("H1",)), "helper": (("V2",), ("N0",), ("N1",))}
+NB = 6
 
 SCRATCH = {"EXL": ("dram", [N, 128, 4], "int32")}
 for _t, _bufs in {
     "int32": {"E4": 4, "EXS": (72, 64), "pco": 1, "ai": 1, "qi": 1, "qci": 1},
-    "float32": {"X": 512, "PA": NV * BLK, "PH": NV * BLK, "PD": 2 * BLK, "LAND": ZERO + 4, "Y0": 2 * CAP,
+    "float32": {"X": 512, "PK": NB * BLK, "PR": NB * BLK, "LAND": ZERO + 4, "Y0": 2 * CAP,
                 "a16": 1, "a16p": 1, "a64": 1, "kc": 1, "jt": 4, "c32": 72, "c128": (1, 72), "on1": (1, 128), "m128": (1, 2),
                 "msk": 72, "e4f": 4, "sc": 72, "hh": 4, "onf": (72, 16), "qif": 1, "mcu": (72, 128), "mcn": (72, 128),
                 "prow": 32, "pc": 32, "qcf": 1, "qc2": 1, "ohr": (72, 128), "cn": (72, 2)},
@@ -26,10 +27,10 @@ for _t, _bufs in {
         SCRATCH[_n] = ("sbuf", list(_s) if isinstance(_s, tuple) else [128, _s], _t)
 for _n in ("psP", "psG", "psC", "psW", "psO"):
     SCRATCH[_n] = ("psum", [128, 512], "float32")
-_K = ["pk%d" % i for i in range(NV + 1)]
-_B = ["b%d" % i for i in range(NV)]
+_K = ["pk%d" % i for i in range(NB)]
+_B = ["b%d" % i for i in range(NB)]
 _AB = ["ab%d" % i for i in range(4)]
-SEMAPHORES = (["le4", "lx", "lex", "lexs", "ls", "exa", "arr", "sty", "yg", "own"]
+SEMAPHORES = (["le4", "lx", "lex", "lexs", "ls", "exa", "arr", "sty", "yg", "own", "hx", "hl"]
               + ["v%d" % i for i in range(17)] + ["r%d" % i for i in range(9)] + ["g%d" % i for i in range(8)]
               + ["p%d" % i for i in range(4)] + _K + _B + _AB)
 _PLANS = {}
@@ -39,8 +40,15 @@ def plan(topo, cores):
     if "plan" in _PLANS:
         return _PLANS["plan"]
     far = lambda a, b: topo.rack(topo.host(a)) != topo.rack(topo.host(b))
+    chip = lambda c: (topo.host(c), topo.chip(c))
+    relay = lambda f, j: ("agent " if j[0] == "V" else "porter ") + f if j[0] in "Vnh" else None
     hosts = sorted(set(topo.host(c) for c in cores))
-    nk, nh = len(KINDS), len(hosts)
+    roles = ["helper"]
+    for f in WORK:
+        for call in WORK[f]:
+            for j in call:
+                if relay(f, j) and relay(f, j) not in roles:
+                    roles.append(relay(f, j))
 
     def ports(k, o):
         hk, ho, ck, co, die = topo.host(k), topo.host(o), topo.chip(k), topo.chip(o), topo.die(k)
@@ -51,47 +59,71 @@ def plan(topo, cores):
             return w, w
         return (("out", ho, ck, die), ("in", ho, co, die)), (("out", hk, ck, die), ("in", hk, co, die))
 
-    serve, cand, use = [], {}, {}
+    out, cand, index, loads = [], {}, {}, {}
+
+    def load(key, k, ds):
+        v = loads.setdefault(key, np.zeros((2, 256)))
+        for d in ds:
+            for w, way in enumerate(ports(k, cores[d])):
+                for e in way:
+                    v[w, index.setdefault(e, len(index))] += 1
+
     for r, c in enumerate(cores):
         fs = sorted((d for d in range(N) if far(cores[d], c)), key=lambda d: (topo.may_write(c, cores[d]), d))
         via = sorted(fs[:NV])
         here = [d for d in range(N) if d != r and topo.host(cores[d]) == topo.host(c)]
         near = [d for d in range(N) if d != r and d not in via and d not in here]
         turn = lambda ds: [ds[(i + r) % len(ds)] for i in range(len(ds))]
-        serve.append({"via": turn(via), "near": turn(near), "here": sorted(here, key=lambda d: (d - r) % N)})
-        use[r] = [ports(c, cores[d]) for d in here]
-        for kind, ds in KINDS:
+        blocks = {"V": turn(via), "N": turn(near), "H": sorted(here, key=lambda d: (d - r) % N)}
+        p = {"work": {}, "serve": {}}
+        for f in WORK:
+            p["work"][f] = [[(blocks[j[0].upper()][int(j[1])], relay(f, j)) for j in call] for call in WORK[f]]
+            p["serve"].setdefault(f, [])
+            for call in p["work"][f]:
+                for d, v in call:
+                    p["serve"].setdefault(v or f, []).append(d)
+        out.append(p)
+        load((r, "rank", 0), c, p["serve"]["rank"])
+        for role in roles:
             for k in range(512):
                 if (topo.chip(k) == topo.chip(c) and k not in cores and topo.may_write(c, k)
-                        and all(topo.may_write(k, cores[d]) for d in serve[r][ds])
-                        and (far(k, c) if kind == "agent" else topo.host(k) == topo.host(c))):
-                    cand.setdefault((r, kind, int(topo.die(k) != topo.die(c))), []).append(k)
+                        and all(topo.may_write(k, cores[d]) for d in p["serve"][role] if role != "helper")
+                        and (far(k, c) if role.startswith("agent") else topo.host(k) == topo.host(c))):
+                    cand.setdefault((r, role, int(topo.die(k) != topo.die(c))), []).append(k)
             for o in (0, 1):
-                use[r, kind, o] = [ports(cand[r, kind, o][0], cores[d]) for d in serve[r][ds]]
+                load((r, role, o), cand[r, role, o][0], p["serve"][role])
+    keys = [(r, role) for r in range(N) for role in roles]
+    fixed = sum(loads[r, "rank", 0] for r in range(N))
+
+    def cost(pick):
+        v = fixed + sum(loads[key + (o,)] for key, o in zip(keys, pick))
+        return v.max(), (v ** 2).sum()
+
     best = None
-    for pick in np.ndindex(*([2] * (nk * nh))):
-        loads = ({}, {})
-        for r, c in enumerate(cores):
-            ws = list(use[r])
-            for i in range(nk):
-                ws += use[r, KINDS[i][0], pick[i * nh + hosts.index(topo.host(c))]]
-            for w in ws:
-                for load, way in zip(loads, w):
-                    for e in way:
-                        load[e] = load.get(e, 0) + 1
-        every = [v for load in loads for v in load.values()]
-        cost = (max(every), sum(pick[nh:]), sum(v * v for v in every))
-        if best is None or cost < best[0]:
-            best = (cost, pick)
-    used, out = set(), []
-    for r, c in enumerate(cores):
-        p = dict(serve[r])
-        for i in range(nk):
-            kind = KINDS[i][0]
-            ks = [k for k in cand[r, kind, best[1][i * nh + hosts.index(topo.host(c))]] if k not in used]
-            p[kind] = ks[-1] if kind == "helper" else ks[0]
-            used.add(p[kind])
-        out.append(p)
+    kinds = [(h, role) for h in hosts for role in roles]
+    rng = np.random.default_rng(1)
+    for start in range(40):
+        st = dict(zip(kinds, rng.integers(0, 2, len(kinds)).tolist()))
+        pick = [0 if role == "helper" else st[topo.host(cores[r]), role] for r, role in keys]
+        now, moved = cost(pick), True
+        while moved:
+            moved = False
+            for i in range(len(keys)):
+                if keys[i][1] != "helper":
+                    p = [o ^ (n == i) for n, o in enumerate(pick)]
+                    c = cost(p)
+                    if c < now:
+                        pick, now, moved = p, c, True
+        if best is None or now < best[0]:
+            best = (now, pick)
+    die = dict(zip(keys, best[1]))
+    used = set()
+    for r in range(N):
+        for role in roles:
+            ks = [k for k in cand[r, role, die[r, role]] if k not in used]
+            busy = [k for k in used | set(cores) if chip(k) == chip(ks[0])]
+            out[r][role] = ks[0] if role.startswith("agent") else max(ks, key=lambda k: min(abs(k - b) for b in busy))
+            used.add(out[r][role])
     _PLANS["plan"] = out
     return out
 
@@ -102,8 +134,9 @@ def rank_program(g, core, T, topo):
     rank = T.rank_of(core)
     relays = {}
     for s, p in enumerate(P):
-        relays[p["agent"]] = (s, p["via"], p["via"], "PA")
-        relays[p["helper"]] = (s, p["near"], p["near"] + p["here"], "PH")
+        for role in p["serve"]:
+            if role != "rank":
+                relays[p[role]] = (s, role)
     if rank is None and core not in relays:
         return
 
@@ -140,9 +173,11 @@ def rank_program(g, core, T, topo):
     def size(m):
         return bin(m).count("1")
 
-    def halves(m):
+    def parts(m, n):
+        if n < 2:
+            return [m][:n]
         bits = [1 << i for i in range(m.bit_length()) if m >> i & 1]
-        return sum(bits[:len(bits) // 2]), sum(bits[len(bits) // 2:])
+        return [q for h in (bits[:len(bits) // 2], bits[len(bits) // 2:]) for q in parts(sum(h), n // 2)]
 
     def send(*trs):
         g.remote_dma_fused([RemoteDMATransfer(dst_ids=ids(ds), dma_engine_mask=m, remote_sem=T.sem[sem], srcs=[src],
@@ -157,27 +192,75 @@ def rank_program(g, core, T, topo):
             m = m & topo.mask(c, d)
         return m
 
-    def masks(s):
-        m = common(cores[s], [P[s]["agent"]] + [cores[d] for d in P[s]["here"]])
-        return m, topo.mask(cores[s], P[s]["helper"]) & ~m
+    def every(s):
+        return topo.mask(cores[s], P[s]["helper"])
+
+    def leave(s):
+        return common(cores[s], [cores[d] for d in range(N) if topo.host(cores[d]) == topo.host(cores[s]) and d != s])
+
+    def calls(s, f):
+        res, n = [], 0
+        for call in P[s]["work"][f]:
+            on = [i for i, (d, v) in enumerate(call) if v and v.startswith("porter")]
+            off = [i for i in range(len(call)) if i not in on]
+            ms = dict(zip(off + on, parts(leave(s), len(off)) + parts(every(s) & ~leave(s), len(on))))
+            res.append([(d, v, n + i, ms[i]) for i, (d, v) in enumerate(call)])
+            n += len(call)
+        return res
+
+    def readers(s, role):
+        return P[s]["serve"][role] + (P[s]["serve"]["rank"] if role == "porter rank" else [])
+
+    def list_mask(s):
+        return parts(leave(s), 2)[0]
+
+    def block(buf, n):
+        return T[buf][:, BLK * n:BLK * n + BLK]
+
+    def vget(out, d, sem):
+        inc(V.tensor_copy(out, T["X"][:].indirect(T["lst"][:, 8 * d:8 * d + 8])), sem)
+
+    def sget(out, d, sem):
+        inc(S.activation(out, T["X"][:].indirect(T["lst"][:, 8 * d:8 * d + 8]), Copy, bias=-0.0), sem)
+
+    def work(s, f):
+        for call in calls(s, f):
+            for d, v, n, m in call:
+                (vget, sget)[n % 2](block("PK", n), d, _K[n])
+        for call in calls(s, f):
+            trs = []
+            for d, v, n, m in call:
+                wait(g, _K[n])
+                if v:
+                    i = P[s]["serve"][v].index(d)
+                    trs.append(([P[s][v]], block("PR", i), block("PK", n), _B[i], m))
+                else:
+                    trs.append(([cores[d]], block("LAND", s), block("PK", n), "arr", m))
+            send(*trs)
 
     if rank is None:
-        src, dests, readers, buf = relays[core]
-        em = common(core, [cores[d] for d in readers])
-        leave, stay = masks(src)
-        expect("exa", size(halves(leave)[0]))
+        src, role = relays[core]
+        em = common(core, [cores[d] for d in readers(src, role)] if role != "helper" else [cores[d] for d in P[src]["serve"][role]])
+        expect("exa", size(list_mask(src)))
         wait(g, "exa")
-        send(([cores[d] for d in readers], T["EXL"][src], T["EXL"][src], "exa", em))
-        for n, d in enumerate(dests):
-            expect(_B[n], size(leave if buf == "PA" else stay))
-            wait(g, _B[n])
-            send(([cores[d]], T["LAND"][:, BLK * src:BLK * src + BLK], T[buf][:, BLK * n:BLK * n + BLK], "arr", em))
+        send(([cores[d] for d in readers(src, role)], T["EXL"][src], T["EXL"][src], "exa", em))
+        if role == "helper":
+            expect("hx", size(every(src)))
+            expect("hl", size(every(src)))
+            for q in (V, S):
+                wait(q, "hx", "hl")
+            work(src, role)
+        else:
+            for f in WORK:
+                for call in calls(src, f):
+                    for d, v, n, m in call:
+                        if v == role:
+                            i = P[src]["serve"][role].index(d)
+                            expect(_B[i], size(m))
+                            wait(g, _B[i])
+                            send(([cores[d]], block("LAND", src), block("PR", i), "arr", em))
         finish()
         return
-
-    me = P[rank]
-    ag, he = me["agent"], me["helper"]
-    leave, stay = masks(rank)
 
     def iota(name, pattern, base, mult, sem):
         inc(g.iota(T[name][:], pattern, base, mult, allow_small_or_imprecise_dtypes=True), sem)
@@ -189,15 +272,19 @@ def rank_program(g, core, T, topo):
             inc(V.tensor_scalar(out, in0, s1, s2, op0, op1), sem)
 
     for k in relays:
-        s, dests, readers, buf = relays[k]
-        n = size(common(k, [cores[d] for d in readers]))
-        if rank in readers:
+        s, role = relays[k]
+        ds = readers(s, role)
+        n = size(common(k, [cores[d] for d in ds]))
+        if rank in ds:
             expect("exa", n)
-        if rank in dests:
+        if rank in P[s]["serve"][role] and role != "helper":
             expect("arr", n)
     for s in range(N):
-        if rank in P[s]["here"]:
-            expect("arr", size(halves(masks(s)[0])[0]))
+        for f in WORK:
+            for call in calls(s, f):
+                for d, v, n, m in call:
+                    if d == rank and not v:
+                        expect("arr", size(m))
     inc(Y.dma_start(T["E4"][:], T["ex"][:]), "le4", 16)
     inc(S.dma_start(T["EXL"][rank], T["ex"][:]), "lex", 16)
     inc(Y.dma_start(T["X"][:], T["x"][:]), "lx", 16)
@@ -206,8 +293,11 @@ def rank_program(g, core, T, topo):
     iota("kap", [[1, 16], [16, 8]], 0, 0, "g1")
     iota("kro", [[1, 18]], 0, 0, "g2")
     iota("aro", [[0, 8], [2, 16]], -15, 0, "g5")
+    me = P[rank]
     wait(g, "lex")
-    send(([ag, he], T["EXL"][rank], T["EXL"][rank], "exa", halves(leave)[0]))
+    send(([me[role] for role in me["serve"] if role != "rank"], T["EXL"][rank], T["EXL"][rank], "exa", list_mask(rank)))
+    wait(g, "lx")
+    send(([me["helper"]], T["X"][:], T["X"][:], "hx", every(rank)))
 
     inc(V.memset(T["msk"][:], 1.0), "v1")
     inc(V.memset(T["c128"][:], 128.0), "v7")
@@ -269,29 +359,12 @@ def rank_program(g, core, T, topo):
     wait(V, "p1")
     inc(V.tensor_copy(T["lst"][:], pg[:, 0:72]), "v14")
 
-    def vget(out, d, sem):
-        inc(V.tensor_copy(out, T["X"][:].indirect(T["lst"][:, 8 * d:8 * d + 8])), sem)
-
-    def sget(out, d, sem):
-        inc(S.activation(out, T["X"][:].indirect(T["lst"][:, 8 * d:8 * d + 8]), Copy, bias=-0.0), sem)
-
-    def block(buf, n):
-        return T[buf][:, BLK * n:BLK * n + BLK]
-
+    wait(g, "v14")
+    send(([me["helper"]], T["lst"][:], T["lst"][:], "hl", every(rank)))
     wait(V, "v14", "lx")
     wait(S, "v14", "lx")
-    for n in range(NV):
-        pa, ph = block("PA", n), block("PH", n)
-        vget(pa, me["via"][n], _K[n])
-        sget(ph, me["near"][n], _K[n])
-        wait(g, _K[n])
-        send(([ag], pa, pa, _B[n], leave), ([he], ph, ph, _B[n], stay))
-    for n, get in enumerate((vget, sget)):
-        get(block("PD", n), me["here"][n], _K[NV])
-    wait(g, _K[NV])
-    own = block("LAND", rank)
-    send(*[([cores[d]], own, block("PD", n), "arr", m) for n, (d, m) in enumerate(zip(me["here"], halves(leave)))])
-    vget(own, rank, "own")
+    work(rank, "rank")
+    vget(block("LAND", rank), rank, "own")
 
     iota("gro", [[1, 8], [0, 16]], 0, 0, "g6")
     iota("prow", [[0, 2], [16, 16]], 0, 0, "g6")

import numpy as np
from concourse.bass import DstId, RemoteDMATransfer
from concourse.mybir import AluOpType, ActivationFunctionType, AxisListType

N, EL, CAP = 9, 2, 240
BLK = 128
ZERO = N * BLK
NV = 3
MAGIC = 1.5 * 2.0 ** 28
BIG = 4096.0
WORK = {"rank": (("V0", "h0"), ("V1", "n2"), ("H1",)), "helper": (("V2",), ("N0",), ("N1",))}
NB = 6

SCRATCH = {"EXL": ("dram", [N, 128, 4], "int32")}
for _t, _bufs in {
    "int32": {"E4": 4, "EXS": (72, 64), "pco": 1, "ai": 1, "qi": 1, "qci": 1},
    "float32": {"X": 512, "PK": NB * BLK, "PR": NB * BLK, "LAND": ZERO + 4, "Y0": 2 * CAP,
                "a16": 1, "a16p": 1, "a64": 1, "kc": 1, "jt": 4, "c32": 72, "c128": (1, 72), "on1": (1, 128), "m128": (1, 2),
                "msk": 72, "e4f": 4, "sc": 72, "hh": 4, "onf": (72, 16), "qif": 1, "mcu": (72, 128), "mcn": (72, 128),
                "prow": 32, "pc": 32, "qcf": 1, "qc2": 1, "ohr": (72, 128), "cn": (72, 2)},
    "bfloat16": {"kap": 128, "kro": 18, "krk": (1, 72), "m15": (1, 72), "aro": 128, "bro": 72, "onb": (1, 128), "meq": 128,
                 "dia": 128, "mle": 128, "mlt": 128, "oh": 72, "gro": 128, "brow": (1, 32), "rr": 128, "th": 32, "th9": (16, 32)},
    "float16": {"bm": 288, "am": 512},
    "uint16": {"lst": 72, "yl": 32},
}.items():
    for _n, _s in _bufs.items():
        SCRATCH[_n] = ("sbuf", list(_s) if isinstance(_s, tuple) else [128, _s], _t)
for _n in ("psP", "psG", "psC", "psW", "psO"):
    SCRATCH[_n] = ("psum", [128, 512], "float32")
_K = ["pk%d" % i for i in range(NB)]
_B = ["b%d" % i for i in range(NB)]
_AB = ["ab%d" % i for i in range(4)]
SEMAPHORES = (["le4", "lx", "lex", "lexs", "ls", "exa", "arr", "sty", "yg", "own", "hx", "hl"]
              + ["v%d" % i for i in range(17)] + ["r%d" % i for i in range(9)] + ["g%d" % i for i in range(8)]
              + ["p%d" % i for i in range(4)] + _K + _B + _AB)
_PLANS = {}


def plan(topo, cores):
    if "plan" in _PLANS:
        return _PLANS["plan"]
    far = lambda a, b: topo.rack(topo.host(a)) != topo.rack(topo.host(b))
    chip = lambda c: (topo.host(c), topo.chip(c))
    relay = lambda f, j: ("agent " if j[0] == "V" else "porter ") + f if j[0] in "Vnh" else None
    hosts = sorted(set(topo.host(c) for c in cores))
    roles = ["helper"]
    for f in WORK:
        for call in WORK[f]:
            for j in call:
                if relay(f, j) and relay(f, j) not in roles:
                    roles.append(relay(f, j))

    def ports(k, o):
        hk, ho, ck, co, die = topo.host(k), topo.host(o), topo.chip(k), topo.chip(o), topo.die(k)
        if ck == co and (hk == ho or far(k, o)):
            return (), ()
        if not far(k, o):
            w = (("out", hk, ck, die), ("in", ho, co, die))
            return w, w
        return (("out", ho, ck, die), ("in", ho, co, die)), (("out", hk, ck, die), ("in", hk, co, die))

    out, cand, index, loads = [], {}, {}, {}

    def load(key, k, ds):
        v = loads.setdefault(key, np.zeros((2, 256)))
        for d in ds:
            for w, way in enumerate(ports(k, cores[d])):
                for e in way:
                    v[w, index.setdefault(e, len(index))] += 1

    for r, c in enumerate(cores):
        fs = sorted((d for d in range(N) if far(cores[d], c)), key=lambda d: (topo.may_write(c, cores[d]), d))
        via = sorted(fs[:NV])
        here = [d for d in range(N) if d != r and topo.host(cores[d]) == topo.host(c)]
        near = [d for d in range(N) if d != r and d not in via and d not in here]
        turn = lambda ds: [ds[(i + r) % len(ds)] for i in range(len(ds))]
        blocks = {"V": turn(via), "N": turn(near), "H": sorted(here, key=lambda d: (d - r) % N)}
        p = {"work": {}, "serve": {}}
        for f in WORK:
            p["work"][f] = [[(blocks[j[0].upper()][int(j[1])], relay(f, j)) for j in call] for call in WORK[f]]
            p["serve"].setdefault(f, [])
            for call in p["work"][f]:
                for d, v in call:
                    p["serve"].setdefault(v or f, []).append(d)
        out.append(p)
        load((r, "rank", 0), c, p["serve"]["rank"])
        for role in roles:
            for k in range(512):
                if (topo.chip(k) == topo.chip(c) and k not in cores and topo.may_write(c, k)
                        and all(topo.may_write(k, cores[d]) for d in p["serve"][role] if role != "helper")
                        and (far(k, c) if role.startswith("agent") else topo.host(k) == topo.host(c))):
                    cand.setdefault((r, role, int(topo.die(k) != topo.die(c))), []).append(k)
            for o in (0, 1):
                load((r, role, o), cand[r, role, o][0], p["serve"][role])
    keys = [(r, role) for r in range(N) for role in roles]
    fixed = sum(loads[r, "rank", 0] for r in range(N))

    def cost(pick):
        v = fixed + sum(loads[key + (o,)] for key, o in zip(keys, pick))
        return v.max(), (v ** 2).sum()

    best = None
    kinds = [(h, role) for h in hosts for role in roles]
    rng = np.random.default_rng(1)
    for start in range(40):
        st = dict(zip(kinds, rng.integers(0, 2, len(kinds)).tolist()))
        pick = [0 if role == "helper" else st[topo.host(cores[r]), role] for r, role in keys]
        now, moved = cost(pick), True
        while moved:
            moved = False
            for i in range(len(keys)):
                if keys[i][1] != "helper":
                    p = [o ^ (n == i) for n, o in enumerate(pick)]
                    c = cost(p)
                    if c < now:
                        pick, now, moved = p, c, True
        if best is None or now < best[0]:
            best = (now, pick)
    die = dict(zip(keys, best[1]))
    used = set()
    for r in range(N):
        for role in roles:
            ks = [k for k in cand[r, role, die[r, role]] if k not in used]
            busy = [k for k in used | set(cores) if chip(k) == chip(ks[0])]
            out[r][role] = ks[0] if role.startswith("agent") else max(ks, key=lambda k: min(abs(k - b) for b in busy))
            used.add(out[r][role])
    _PLANS["plan"] = out
    return out


def rank_program(g, core, T, topo):
    cores = list(T.cores)
    P = plan(topo, cores)
    rank = T.rank_of(core)
    relays = {}
    for s, p in enumerate(P):
        for role in p["serve"]:
            if role != "rank":
                relays[p[role]] = (s, role)
    if rank is None and core not in relays:
        return

    V, S, PE, Y = g.vector, g.scalar, g.tensor, g.sync
    A = AluOpType
    Copy = ActivationFunctionType.Copy
    AX = AxisListType.X
    cnt, seen = {}, {}

    def inc(ins, name, n=1):
        ins.then_inc(T.sem[name], n)
        cnt[name] = cnt.get(name, 0) + n

    def wait(q, *names):
        for name in names:
            q.wait_ge(T.sem[name], cnt[name])
            seen[name] = cnt[name]

    def expect(name, n):
        cnt[name] = cnt.get(name, 0) + n

    def finish():
        for name in sorted(cnt):
            if seen.get(name, 0) < cnt[name]:
                wait(g, name)

    def ids(ds):
        res = []
        for d in ds:
            rid, pid = topo.addr(d, core)
            res.append(DstId(rid=rid, pnc=pid))
        return res

    def size(m):
        return bin(m).count("1")

    def parts(m, n):
        if n < 2:
            return [m][:n]
        bits = [1 << i for i in range(m.bit_length()) if m >> i & 1]
        return [q for h in (bits[:len(bits) // 2], bits[len(bits) // 2:]) for q in parts(sum(h), n // 2)]

    def send(*trs):
        g.remote_dma_fused([RemoteDMATransfer(dst_ids=ids(ds), dma_engine_mask=m, remote_sem=T.sem[sem], srcs=[src],
                                              dsts=[dst for d in ds], alu_op=0) for ds, dst, src, sem, m in trs],
                           local_sem=T.sem["ls"])
        for tr in trs:
            expect("ls", size(tr[4]))

    def common(c, ds):
        m = topo.mask(c, ds[0])
        for d in ds:
            m = m & topo.mask(c, d)
        return m

    def every(s):
        return topo.mask(cores[s], P[s]["helper"])

    def leave(s):
        return common(cores[s], [cores[d] for d in range(N) if topo.host(cores[d]) == topo.host(cores[s]) and d != s])

    def calls(s, f):
        res, n = [], 0
        for call in P[s]["work"][f]:
            on = [i for i, (d, v) in enumerate(call) if v and v.startswith("porter")]
            off = [i for i in range(len(call)) if i not in on]
            ms = dict(zip(off + on, parts(leave(s), len(off)) + parts(every(s) & ~leave(s), len(on))))
            res.append([(d, v, n + i, ms[i]) for i, (d, v) in enumerate(call)])
            n += len(call)
        return res

    def readers(s, role):
        return P[s]["serve"][role] + (P[s]["serve"]["rank"] if role == "porter rank" else [])

    def list_mask(s):
        return parts(leave(s), 2)[0]

    def block(buf, n):
        return T[buf][:, BLK * n:BLK * n + BLK]

    def vget(out, d, sem):
        inc(V.tensor_copy(out, T["X"][:].indirect(T["lst"][:, 8 * d:8 * d + 8])), sem)

    def sget(out, d, sem):
        inc(S.activation(out, T["X"][:].indirect(T["lst"][:, 8 * d:8 * d + 8]), Copy, bias=-0.0), sem)

    def work(s, f):
        for call in calls(s, f):
            for d, v, n, m in call:
                (vget, sget)[n % 2](block("PK", n), d, _K[n])
        for call in calls(s, f):
            trs = []
            for d, v, n, m in call:
                wait(g, _K[n])
                if v:
                    i = P[s]["serve"][v].index(d)
                    trs.append(([P[s][v]], block("PR", i), block("PK", n), _B[i], m))
                else:
                    trs.append(([cores[d]], block("LAND", s), block("PK", n), "arr", m))
            send(*trs)

    if rank is None:
        src, role = relays[core]
        em = common(core, [cores[d] for d in readers(src, role)] if role != "helper" else [cores[d] for d in P[src]["serve"][role]])
        expect("exa", size(list_mask(src)))
        wait(g, "exa")
        send(([cores[d] for d in readers(src, role)], T["EXL"][src], T["EXL"][src], "exa", em))
        if role == "helper":
            expect("hx", size(every(src)))
            expect("hl", size(every(src)))
            for q in (V, S):
                wait(q, "hx", "hl")
            work(src, role)
        else:
            for f in WORK:
                for call in calls(src, f):
                    for d, v, n, m in call:
                        if v == role:
                            i = P[src]["serve"][role].index(d)
                            expect(_B[i], size(m))
                            wait(g, _B[i])
                            send(([cores[d]], block("LAND", src), block("PR", i), "arr", em))
        finish()
        return

    def iota(name, pattern, base, mult, sem):
        inc(g.iota(T[name][:], pattern, base, mult, allow_small_or_imprecise_dtypes=True), sem)

    def ts(sem, out, in0, s1, op0, s2=None, op1=None):
        if op1 is None:
            inc(V.tensor_scalar(out, in0, s1, None, op0), sem)
        else:
            inc(V.tensor_scalar(out, in0, s1, s2, op0, op1), sem)

    for k in relays:
        s, role = relays[k]
        ds = readers(s, role)
        n = size(common(k, [cores[d] for d in ds]))
        if rank in ds:
            expect("exa", n)
        if rank in P[s]["serve"][role] and role != "helper":
            expect("arr", n)
    for s in range(N):
        for f in WORK:
            for call in calls(s, f):
                for d, v, n, m in call:
                    if d == rank and not v:
                        expect("arr", size(m))
    inc(Y.dma_start(T["E4"][:], T["ex"][:]), "le4", 16)
    inc(S.dma_start(T["EXL"][rank], T["ex"][:]), "lex", 16)
    inc(Y.dma_start(T["X"][:], T["x"][:]), "lx", 16)

    inc(g.iota(T["pco"][:], [[0, 1]], 0, 1), "g0")
    iota("kap", [[1, 16], [16, 8]], 0, 0, "g1")
    iota("kro", [[1, 18]], 0, 0, "g2")
    iota("aro", [[0, 8], [2, 16]], -15, 0, "g5")
    me = P[rank]
    wait(g, "lex")
    send(([me[role] for role in me["serve"] if role != "rank"], T["EXL"][rank], T["EXL"][rank], "exa", list_mask(rank)))
    wait(g, "lx")
    send(([me["helper"]], T["X"][:], T["X"][:], "hx", every(rank)))

    inc(V.memset(T["msk"][:], 1.0), "v1")
    inc(V.memset(T["c128"][:], 128.0), "v7")
    inc(V.memset(T["onb"][:], 1.0), "v0")
    inc(V.memset(T["m15"][:], -15.0), "v0")
    wait(V, "v1")
    inc(V.memset(T["msk"][:, 0:72:18], 0.0), "v3")
    wait(V, "g0")
    ts("v2", T["ai"][:], T["pco"][:], 7, A.bitwise_and)
    ts("v2", T["qi"][:], T["pco"][:], 3, A.arith_shift_right)
    inc(V.memset(T["c32"][:], 32.0), "v7")
    wait(V, "v2")
    ts("v4", T["a16"][:], T["ai"][:], 16.0, A.mult)
    ts("v4", T["a16p"][:], T["ai"][:], 16.0, A.mult, 16.0, A.add)
    ts("v4", T["a64"][:], T["ai"][:], 64.0, A.mult)
    wait(V, "v3", "v7")
    inc(V.tensor_tensor_scan(T["krk"][:], T["msk"][0:1, :], T["c128"][:], 0.0, A.mult, A.add), "v15")
    wait(V, "v4", "g1")
    ts("v5", T["kc"][:], T["qi"][:], T["a16"][:], A.add)
    ts("v6", T["mle"][:], T["kap"][:], T["a16"][:], A.is_ge, 2.0, A.mult)
    ts("v6", T["mlt"][:], T["kap"][:], T["a16p"][:], A.is_ge, 2.0, A.mult)
    wait(V, "v5")
    ts("v6", T["meq"][:], T["kap"][:], T["kc"][:], A.is_gt, 2.0, A.mult)
    ts("v6", T["dia"][:], T["kap"][:], T["kc"][:], A.is_equal, BIG, A.mult)

    wait(V, "le4")
    inc(V.tensor_copy(T["e4f"][:], T["E4"][:]), "v9")
    wait(V, "v9", "g2")
    for i in range(4):
        ts("v10", T["oh"][:, 18 * i:18 * i + 18], T["kro"][:], T["e4f"][:, i:i + 1], A.is_equal)
    inc(V.tensor_tensor_scan(T["bro"][:], T["c32"][:], T["c32"][:], BIG + 96.0, A.add, A.max), "v16")
    for i in range(4):
        ts("v8", T["jt"][:, i:i + 1], T["qi"][:], T["a64"][:], A.add, 16.0 * i, A.add)
    ps, oh = T["psP"], T["oh"]
    wait(PE, "v0", "v15")
    PE.matmul(ps[:, 0:72], T["onb"][:], T["krk"][:], True, False)
    PE.matmul(ps[:, 0:72], T["onb"][:], T["m15"][:], False, False)
    wait(PE, "v6", "v10")
    for n in (1, 2, 3):
        PE.matmul(ps[:, 18 * n:72], T["mle"][:], oh[:, 0:72 - 18 * n], False, False)
    for n in (1, 2, 3):
        PE.matmul(ps[:, 0:72 - 18 * n], T["mlt"][:], oh[:, 18 * n:72], False, False)
    PE.matmul(ps[:, 0:72], T["meq"][:], oh[:], False, False)
    inc(PE.matmul(ps[:, 0:72], T["dia"][:], oh[:], False, True), "p0")
    wait(V, "p0")
    inc(V.tensor_tensor_scan(T["sc"][:], T["msk"][:], ps[:, 0:72], 0.0, A.mult, A.max), "v11")
    wait(V, "v11")
    ts("v12", T["hh"][:], T["sc"][:, 17:72:18], MAGIC, A.add, MAGIC, A.subtract)
    wait(V, "v12", "v8", "v16", "g5")
    for i in range(4):
        ts(_AB[i], T["am"][:, 128 * i:128 * i + 128], T["aro"][:], T["hh"][:, i:i + 1], A.add,
           T["sc"][:, 17 + 18 * i:18 + 18 * i], A.is_equal)
        ts(_AB[i], T["bm"][:, 72 * i:72 * i + 72], T["bro"][:], T["hh"][:, i:i + 1], A.is_equal, T["jt"][:, i:i + 1], A.mult)
    pg = T["psG"]
    for i in range(4):
        wait(PE, _AB[i])
        m = PE.matmul(pg[:, 0:72], T["am"][:, 128 * i:128 * i + 128], T["bm"][:, 72 * i:72 * i + 72], i == 0, i == 3)
    inc(m, "p1")
    wait(V, "p1")
    inc(V.tensor_copy(T["lst"][:], pg[:, 0:72]), "v14")

    wait(g, "v14")
    send(([me["helper"]], T["lst"][:], T["lst"][:], "hl", every(rank)))
    wait(V, "v14", "lx")
    wait(S, "v14", "lx")
    work(rank, "rank")
    vget(block("LAND", rank), rank, "own")

    iota("gro", [[1, 8], [0, 16]], 0, 0, "g6")
    iota("prow", [[0, 2], [16, 16]], 0, 0, "g6")
    iota("brow", [[64, 2], [16, 16]], 0, 0, "g6")
    inc(V.memset(T["onf"][:], 1.0), "r0")
    inc(V.memset(T["on1"][:], 1.0), "r0")
    inc(V.memset(T["m128"][:], -128.0), "r0")
    inc(V.memset(T["LAND"][:, ZERO:ZERO + 4], 0.0), "r0")
    ts("r1", T["qci"][:], T["pco"][:], 15, A.bitwise_and)
    inc(V.tensor_copy(T["qif"][:], T["qi"][:]), "r1")
    wait(V, "r1")
    inc(V.tensor_copy(T["qcf"][:], T["qci"][:]), "r2")
    ts("r2", T["qc2"][:], T["qci"][:], 2.0, A.mult, 15.0, A.subtract)
    wait(V, "g6")
    ts("r3", T["mcu"][:], T["gro"][0:72, :], T["qif"][0:72, :], A.is_ge)
    ts("r3", T["mcn"][:], T["gro"][0:72, :], T["qif"][0:72, :], A.is_equal)
    wait(V, "r2")
    ts("r3", T["rr"][:], T["aro"][:], T["qc2"][:], A.is_equal, -1.0, A.mult)
    ts("r3", T["pc"][:], T["prow"][:], T["qcf"][:], A.add)

    wait(Y, "exa", "lex")
    inc(Y.dma_start(T["EXS"][:], T["EXL"][:]), "lexs", 16)
    wait(V, "lexs")
    for e in range(EL):
        ts("r4", T["ohr"][:, 64 * e:64 * e + 64], T["EXS"][:], float(EL * rank + e), A.is_equal)
    wait(V, "r4")
    for e in range(EL):
        inc(V.tensor_reduce(T["cn"][:, e:e + 1], T["ohr"][:, 64 * e:64 * e + 64], AX, A.add), "r5")
    pc_, pw, po = T["psC"], T["psW"], T["psO"]
    wait(PE, "g6", "r0")
    PE.matmul(po[:, 0:32], T["onb"][:], T["brow"][:], True, False)
    PE.matmul(pw[:, 0:2], T["on1"][:], T["m128"][:], True, False)
    wait(PE, "r3", "r5")
    PE.matmul(pw[:, 0:2], T["mcn"][:], T["cn"][:], False, True)
    PE.matmul(pc_[:, 0:2], T["mcu"][:], T["cn"][:], True, True)
    inc(PE.matmul(pc_[0:16, 2:4], T["onf"][:], T["cn"][:], True, True), "p2")
    wait(V, "p2", "r3")
    for e in range(EL):
        ts("r7", T["th9"][:, 16 * e:16 * e + 16], T["pc"][0:16, 16 * e:16 * e + 16], pc_[0:16, 2 + e:3 + e],
           A.is_ge, -float(ZERO), A.mult)
    for e in range(EL):
        ts("r7", T["th"][:, 16 * e:16 * e + 16], T["pc"][:, 16 * e:16 * e + 16], pc_[:, e:e + 1], A.is_ge,
           pw[:, e:e + 1], A.mult)
    wait(PE, "r7")
    PE.matmul(po[:, 0:32], T["rr"][0:16, :], T["th9"][:], False, False)
    inc(PE.matmul(po[:, 0:32], T["rr"][:], T["th"][:], False, True), "p3")
    wait(V, "p3")
    ts("r8", T["yl"][:], po[:, 0:32], T["qcf"][:], A.add, float(ZERO), A.min)

    wait(V, "r8", "own", "arr")
    inc(V.tensor_copy(T["Y0"][:, 0:CAP], T["LAND"][:].indirect(T["yl"][:, 0:15])), "yg")
    wait(S, "r8", "r0", "own", "arr")
    inc(S.activation(T["Y0"][:, CAP:2 * CAP], T["LAND"][:].indirect(T["yl"][:, 16:31]), Copy, bias=-0.0), "yg")
    wait(Y, "yg")
    inc(Y.dma_start(T["y"][:], T["Y0"][:]), "sty", 16)
    finish()
